import numpy as np, ml_dtypes
CORES = [35,38,43,46]
N = 4
BF = ml_dtypes.bfloat16
def gentries(a):
    return np.ascontiguousarray(a.reshape(8, 16, -1).transpose(0, 2, 1)).reshape(8, -1)
def gtable(e):
    e = np.asarray(e); return np.ascontiguousarray(e.reshape(8, -1, 16).transpose(0, 2, 1)).reshape(128, -1).astype(np.int32)
V, L, ST, RO, CAP = 1536, 256, 4, 2, 64
W = V + RO * ST * L
E = 4095
VOID = 2 ** 20
def pack(a, c, x, t, h):
    return {"a0": np.ascontiguousarray(a.reshape(N, 128, V)).astype(np.float32).astype(BF), "kids": np.ascontiguousarray(c.reshape(N, 128, V)).astype(np.int32),
            "x0": np.ascontiguousarray(x.reshape(N, 128, L)).astype(np.float32).astype(BF), "tops": np.stack([gtable(u) for u in t]), "th": np.ascontiguousarray(h).astype(np.int32)}
def near(rng, p, n):
    k = rng.integers(0, 24, (N, 8, 1, n)); z = rng.integers(1, 25, (N, 8, 1, n))
    v = np.take_along_axis(np.broadcast_to(p, (N, 8, 16, 24)), np.broadcast_to(k, (N, 8, 16, n)), 3)
    return np.clip(v + np.rint(z * rng.standard_normal((N, 8, 16, n))), 0, 255).astype(np.int64)
def parts(rng):
    p = rng.integers(0, 256, (8, 16, 24)); p[..., ::3] = rng.integers(0, 40, (8, 16, 8))
    fill = rng.choice(np.array([0.2, 0.5, 0.8, 1.0]), (N, 8, 1, V))
    c = np.where(rng.random((N, 8, 16, V)) < fill, rng.integers(0, V, (N, 8, 16, V)), E)
    hot = np.take_along_axis(rng.integers(0, V, (N, 8, 8)), rng.integers(0, 8, (N, 8, L)), 2)
    t = np.where(rng.random((N, 8, L)) < 0.2, hot, rng.integers(0, V, (N, 8, L)))
    h = np.minimum(rng.choice(np.array([60, 200, 500, 900, 4000]), (N, 8, L)) + rng.integers(0, 100, (N, 8, L)), 4080)
    return near(rng, p, V), c, near(rng, p, L), t, h
def setup_inputs(rng):
    return pack(*parts(rng))
def setup_inputs_spread(rng):
    a = np.minimum(np.exp2(8 * rng.random((N, 8, 1, V))) * rng.random((N, 8, 16, V)), 255).astype(np.int64)
    x = np.minimum(np.exp2(8 * rng.random((N, 8, 1, L))) * rng.random((N, 8, 16, L)), 255).astype(np.int64)
    fill = np.minimum(1.25 * rng.random((N, 8, 1, V)), 1.0)
    c = np.where(rng.random((N, 8, 16, V)) < fill, np.minimum((V * rng.random((N, 8, 16, V)) ** 2).astype(np.int64), V - 1), E)
    t = np.minimum((V * rng.random((N, 8, L)) ** 3).astype(np.int64), V - 1)
    h = np.minimum(np.exp2(12 * rng.random((N, 8, L))).astype(np.int64) - 1, 4080)
    return pack(a, c, x, t, h)
def setup_inputs_ends(rng):
    def both(n):
        k = rng.integers(0, 4, (N, 8, 1, n)); m = 255 * rng.integers(0, 2, (N, 8, 16, n))
        return np.where(k == 0, 0, np.where(k == 1, 255, m))
    a, x = both(V), both(L); a[..., 0] = 255 * rng.integers(0, 2, (N, 8, 16))
    h = 4080 * rng.integers(0, 2, (N, 8, L)); s = (N, 8, 16, V)
    c = np.where(rng.random(s) < 0.5, 0, np.where(rng.random(s) < 0.3, V - 1, rng.integers(0, V, s)))
    c = np.where(rng.random(s) < rng.choice(np.array([0.1, 0.4, 0.6, 1.0]), (N, 8, 1, V)), c, E)
    m = np.argsort(rng.random((N, 8, L)), axis=2) < (2 * L) // 3
    t = np.where(m, (V - 1) * rng.integers(0, 2, (N, 8, L)), rng.integers(1, V - 5, (N, 8, L)))
    t[:, 7] = np.where(m[:, 7], t[:, 7], rng.integers(1, V - 6 - (CAP + 2), (N, L)))
    a[..., V - 1] = 255; a[..., V - 2] = 255; c[..., V - 1] = E; c[..., V - 2] = E
    c[:, :, 2, V - 1] = V - 2; c[:, :, 15, V - 1] = V - 1; c[:, :, 15, V - 2] = V - 1
    a[..., V - 5] = 0; c[..., V - 5] = E; c[:, :, 0, V - 5] = V - 5; c[..., V - 4] = V - 5
    o = t[:, 1::2]; o[o == V - 1] = 0
    for q in range(N):
        i = np.nonzero(~m[q, 7, :L - 2])[0][-(CAP + 2):]; u = V - 6 - np.arange(CAP + 2)
        c[q, 7][:, u] = V - 5; x[q, 7][:, i] = 255; h[q, 7, i] = 0; t[q, 7, i] = u
    x[..., L - 1] = 0; h[..., L - 1] = 4080; t[..., L - 1] = V - 1
    x[..., L - 2] = 255; h[..., L - 2] = 0; t[..., L - 2] = V - 4
    return pack(a, c, x, t, h)
def setup_inputs_corners(rng):
    a = rng.integers(0, 201, (N, 8, 16, V)); x = rng.integers(201, 256, (N, 8, 16, L)); s = (N, 8, 16, V)
    c = np.where(rng.random(s) < rng.choice(np.array([0.1, 0.5, 0.9]), (N, 8, 1, V)), rng.integers(0, V, s), E)
    t = np.zeros((N, 8, L), np.int64); h = np.zeros((N, 8, L), np.int64)
    case = np.array([0, 1, CAP - 1, CAP, CAP + 1, L])[rng.integers(0, 6, (N, 8))]
    case[0] = (CAP, CAP + 1, L, CAP - 1, 1, 0, CAP, CAP + 1); case[1] = (0, L, 1, 0, CAP, CAP + 1, CAP - 1, 0); case[N - 1, 7] = CAP
    for q in range(N):
        for g in range(8):
            n = int(case[q, g]); o = rng.permutation(V); full, leaf, one, more = o[:L], o[L:L + 64], o[L + 64:L + 128], o[L + 128:]; k = c[q, g]
            k[:, full] = rng.integers(0, V, (16, L)); k[:, leaf] = E; k[:, one] = E; k[rng.integers(0, 16, 64), one] = rng.integers(0, V, 64)
            if n == 0: k[15, np.all(k == E, axis=0)] = V - 1
            w = rng.integers(0, 4, L); again = rng.choice(full[:n] if n else one, L)
            u = np.where(w == 0, again, np.where(w == 1, rng.choice(leaf, L), np.where(w == 2, rng.choice(one, L), rng.choice(more, L))))
            y = np.where((w == 0) & (n > 0), 0, 4080); i = rng.permutation(L)[:n]; u[i] = full[:n]; y[i] = 0
            t[q, g] = u; h[q, g] = y
    return pack(a, c, x, t, h)
def half(rng, who, n):
    return np.where(rng.random((16, n)) < 0.5, rng.choice(who, (16, n)), E)
def late(rng, A, C, X, T, H):
    u = rng.permutation(V)[:L // 2]; A[:] = rng.integers(0, 201, (16, V)); X[:] = rng.integers(201, 256, (16, L))
    C[:, u] = rng.integers(0, V, (16, L // 2)); C[rng.integers(0, 16, L // 2), u] = E
    T[:] = np.repeat(u, 2); H[:] = 0
def splits(rng, A, C, X, T, H):
    o = rng.permutation(V); s, b, d, far = o[:L], o[L:L + 16], o[L + 16:L + 32], o[L + 32:]
    A[:, far] = rng.integers(240, 256, (16, far.size)); A[:, b] = rng.integers(200, 211, (16, 16)); A[:, d] = rng.integers(100, 121, (16, 16))
    kb = rng.integers(0, 16, 16); kd = (kb + rng.integers(1, 16, 16)) & 15; w = rng.integers(0, 16, L)
    C[:] = E; C[:, far] = half(rng, far, far.size); C[:, b] = half(rng, far, 16); C[kb, b] = E; C[kd, b] = d
    C[:, s] = half(rng, far, L); C[kd[w], s] = rng.choice(far, L); C[kb[w], s] = b[w]
    X[:] = A[:, d[w]] + rng.integers(0, 3, (16, L)); T[:] = s; H[:] = rng.integers(400, 600, L)
def hosts(rng, A, C, X, T, H):
    o = rng.permutation(V); s, b, far = o[:L], o[L:2 * L], o[2 * L:]
    X[:] = rng.integers(100, 121, (16, L)); A[:, far] = rng.integers(240, 256, (16, far.size)); A[:, b] = X + rng.integers(5, 13, (16, L))
    C[:] = E; C[:, far] = half(rng, far, far.size); C[:, b] = half(rng, far, L); C[:, s] = half(rng, far, L); C[rng.integers(0, 16, L), s] = b
    T[:] = s; H[:] = rng.integers(900, 1100, L)
def made(rng, A, C, X, T, H):
    k = L // 8; o = rng.permutation(V); v, b, s, far = o[:k], o[k:2 * k], o[2 * k:3 * k], o[3 * k:]
    i = rng.permutation(L); pz = np.sort(i[:2 * k].reshape(k, 2), axis=1); p, z, r = pz[:, 0], pz[:, 1], i[2 * k:3 * k]
    n = rng.integers(12, 41, k); m = np.argsort(rng.random((16, k)), axis=0) < 8
    w = np.argsort(rng.random((16, k)), axis=0)[:3]; w[:2] = np.sort(w[:2], axis=0)
    A[:, far] = rng.integers(240, 256, (16, far.size)); A[:, b] = np.where(m, n, 0); A[:, s] = np.where(m, n, 2 * n)
    C[:] = E; C[:, far] = half(rng, far, far.size); C[w[0], v] = b; C[w[1], v] = s
    C[:, b] = rng.choice(far, (16, k)); C[w[2], b] = E
    T[:] = rng.choice(far, L); T[p] = v; T[z] = v; T[r] = b
    y = np.where(m, 2 * n, n); X[:, p] = y; X[:, z] = n; X[:, r] = y + rng.integers(1, 4, (16, k))
    H[p] = 12 * n; H[z] = 0; H[r] = 0
def setup_inputs_ties(rng):
    a = 100 * (rng.random((N, 8, 1, V)) < 0.6) + rng.integers(0, 3, (N, 8, 16, V)) * (rng.random((N, 8, 1, V)) < 0.8)
    x = 100 + rng.integers(0, 3, (N, 8, 16, L)) * (rng.random((N, 8, 1, L)) < 0.8); s = (N, 8, 16, V)
    c = np.where(rng.random(s) < 0.5, rng.integers(0, 64, s), rng.integers(0, V, s))
    c = np.where(rng.random(s) < rng.choice(np.array([0.2, 0.6, 0.9, 1.0]), (N, 8, 1, V)), c, E)
    h = np.where(rng.random((N, 8, L)) < 0.8, rng.integers(0, 20, (N, 8, L)), 1600)
    t = rng.integers(0, V, (N, 8, L))
    for q in range(N):
        for g, fn in ((1, late), (2, splits), (4, hosts), (6, made)):
            if g == 1 or q % 2 == 0: fn(rng, a[q, g], c[q, g], x[q, g], t[q, g], h[q, g])
    return pack(a, c, x, t, h)
def setup_inputs_alike(rng):
    a, c, x, t, h = parts(rng)
    c[:, 0] = rng.integers(0, V, (N, 1, V)); c[:, 1] = np.where(c[:, 1] == E, E, np.arange(V))
    t[:, 2] = rng.integers(0, V, (N, 1)); t[:, 3] = np.where(rng.random((N, L)) < 0.5, rng.integers(0, V, (N, 1)), V - 1)
    c[:, 4] = np.where(c[:, 4] == E, E, rng.choice(np.array([0, 5, V - 1]), (N, 16, V)))
    a[:, 5] = np.minimum(a[:, 5], 200); c[:, 5] = rng.integers(0, V, (N, 16, V)); t[:, 5] = np.arange(L) % CAP
    x[:, 5] = rng.integers(201, 256, (N, 16, L)); h[:, 5] = 0
    x[:, 6] = x[:, 6, :, :1]
    c[:, 7] = rng.integers(0, V, (N, 16, V))
    return pack(a, c, x, t, h)
def check_inputs(d):
    bad = []
    for k, lo, hi in (("a0", 0, 255), ("kids", 0, E), ("x0", 0, 255), ("tops", 0, V - 1), ("th", 0, 4080)):
        v = np.asarray(d[k]).astype(np.float64)
        if not (np.min(v) >= lo and np.max(v) <= hi) or np.any(v != np.floor(v)): bad.append("range of " + k)
        elif k == "kids" and np.any((v >= V) & (v != E)): bad.append("range of " + k)
    return bad
def first(key, on):
    k = np.where(on, key, 8192 + np.arange(L)); o = np.argsort(k, axis=1, kind="stable"); s = np.take_along_axis(k, o, 1)
    m = np.ones(k.shape, bool); m[:, 1:] = s[:, 1:] != s[:, :-1]
    r = np.zeros(k.shape, bool); np.put_along_axis(r, o, m, 1)
    return r & on
def pick(t, i):
    return t[np.arange(t.shape[0]).reshape((-1,) + (1,) * (i.ndim - 1)), i]
def at(t, k):
    return np.take_along_axis(t, k[..., None], 2)[..., 0]
def reference(a0, kids, x0, tops, th):
    B = 8 * N
    A = np.zeros((B, W, 16), np.int32); A[:, :V] = a0.astype(np.float32).astype(np.int32).reshape(B, 16, V).transpose(0, 2, 1)
    C = np.full((B, W, 16), E, np.int32); C[:, :V] = kids.reshape(B, 16, V).transpose(0, 2, 1)
    x = np.ascontiguousarray(x0.astype(np.float32).astype(np.int32).reshape(B, 16, L).transpose(0, 2, 1))
    top = np.stack([gentries(u) for u in tops]).astype(np.int64).reshape(B, L); lim = th.reshape(B, L).astype(np.int32)
    for rnd in range(RO):
        v = top.copy(); rest = np.zeros((B, L), bool)
        come = np.zeros((N, 8, ST * CAP, 16), np.int32); ok = np.zeros((N, 8, ST * CAP), bool)
        for j in range(ST):
            sg = rnd * ST + j; act = first(v, ~rest)
            c = pick(C, v); filled = c != E
            e = np.where(filled, np.add.reduce(np.abs(x[:, :, None] - pick(A, np.where(filled, c, 0))), axis=3), VOID)
            kb = np.argmin(e, axis=2); eb = at(e, kb); e2 = e.copy(); np.put_along_axis(e2, kb[..., None], VOID, 2)
            kq = np.argmin(e2, axis=2); eq = at(e2, kq)
            b = np.where(eb < VOID, at(c, kb), 0); q = np.where(eq < VOID, at(c, kq), 0)
            ab = pick(A, b); mid = (ab + pick(A, q)) >> 1
            em = np.where(eq < VOID, np.add.reduce(np.abs(x - mid), axis=2), VOID)
            d = np.where((eb < VOID)[..., None], pick(C, b), E)
            f = np.where(d != E, np.add.reduce(np.abs(x[:, :, None] - pick(A, np.where(d != E, d, 0))), axis=3), VOID)
            w = np.argmin(np.stack([eb, em, np.min(f, axis=2), lim], axis=2), axis=2)
            host, merge, split, new = [act & (w == u) for u in range(4)]
            empty = ~filled; room = np.any(empty, axis=2); k0 = np.argmax(empty, axis=2); over = new & ~room
            n = V + L * sg + np.arange(L)
            g, i = np.nonzero(host & first(b, host))
            A[g, b[g, i]] = ab[g, i] + np.clip(x[g, i] - ab[g, i], -4, 4)
            g, i = np.nonzero(merge)
            A[g, n[i]] = mid[g, i]; C[g, n[i], kb[g, i]] = b[g, i]; C[g, n[i], kq[g, i]] = q[g, i]
            C[g, v[g, i], kb[g, i]] = n[i]; C[g, v[g, i], kq[g, i]] = E
            g, i = np.nonzero(split)
            t = c[g, i]; t[np.arange(len(g)), kb[g, i]] = E; C[g, v[g, i]] = np.where(t == E, d[g, i], t)
            g, i = np.nonzero(new & room)
            A[g, n[i]] = x[g, i]; C[g, v[g, i], k0[g, i]] = n[i]
            v = np.where(host, b, np.where(merge, n, v)); rest = rest | new
            pl = np.add.accumulate(over.astype(np.int64), axis=1) - 1; g, i = np.nonzero(over & (pl < CAP))
            to = (g // 8 + 1 + sg % (N - 1)) % N
            come[to, g % 8, j * CAP + pl[g, i]] = x[g, i]; ok[to, g % 8, j * CAP + pl[g, i]] = True
        ok = ok.reshape(B, ST * CAP); come = pick(come.reshape(B, ST * CAP, 16), np.argsort(~ok, axis=1, kind="stable"))
        cnt = np.add.reduce(ok.astype(np.int64), axis=1)[:, None]; nr = np.add.accumulate(rest.astype(np.int64), axis=1) - 1
        got = rest & (nr < cnt)
        x = np.where(got[..., None], pick(come, np.clip(nr, 0, ST * CAP - 1)), np.abs(x - pick(A, v)))
    return {"ya": np.ascontiguousarray(A.transpose(0, 2, 1)).reshape(N, 128, W).astype(np.float32).astype(BF),
            "yc": np.ascontiguousarray(C.transpose(0, 2, 1)).reshape(N, 128, W).astype(np.float32),
            "yx": np.ascontiguousarray(x.transpose(0, 2, 1)).reshape(N, 128, L).astype(np.float32).astype(BF)}

@@ -1,0 +1,801 @@
+from concourse.bass import DstId, RemoteDMATransfer
+from concourse.mybir import dt, AluOpType, ActivationFunctionType
+OP = AluOpType
+AF = ActivationFunctionType
+B2, F4, H2, I4, U2 = "bfloat16", "float32", "float16", "int32", "uint16"
+BIG = 1.0e9
+PEC, WAKE = 0.52, 75.0
+PRI = {"sl": 1500, "em": 3000, "ql": 6000, "bg": 3000, "sg": -1500, "v21": -1500, "v20": 1500}
+TOT = [0.0]
+SCRATCH = {}
+
+
+PART = {}
+
+
+def sb(dtype, n, *names):
+    if len(names) > 2 and n <= 256:
+        big = "w%d%s" % (n, dtype)
+        SCRATCH[big] = ("sbuf", [128, n * len(names)], dtype)
+        for j, k in enumerate(names):
+            PART[k] = (big, n * j, n)
+    else:
+        for k in names:
+            SCRATCH[k] = ("sbuf", [128, n], dtype)
+
+
+def info(name):
+    return SCRATCH[PART[name][0] if name in PART else name]
+
+
+sb(B2, 4096, "A", "X16", "E", "IND")
+sb(F4, 4096, "C")
+sb(B2, 512, "G")
+sb(B2, 2048, "ONE", "BC", "BA", "BB", "TB")
+sb(B2, 128, "BLK", "ID", "IN", "IN2", "I4K", "IN128", "IN16", "I512", "IN512", "IN256", "TN", "T2", "TA", "CK", "CM128", "CMH", "KW", "S00", "S01", "S10", "S11")
+sb(B2, 144, "Z1", "Z16")
+sb(B2, 256, "X")
+sb(B2, 256, "KC", "LOI", "EM", "M2", "AM", "AB", "CLP", "SBN", "SQN", "CNM", "AV", "AQ", "nB", "nN")
+sb(F4, 256, "NB0", "NBS", "RS", "RS2", "ct", "dtf", "m1", "m2", "m3", "zz", "c2", "yy", "selc", "tmpf", "yB", "sB")
+sb(H2, 256, "ZQ", "cH")
+sb(U2, 256, "cU", "dU", "vBU")
+sb(I4, 1536, "KI")
+sb(F4, 768, "CC")
+sb(F4, 512, "CN")
+sb(B2, 768, "CA")
+sb(F4, 16, "il", "nF", "vact", "TR", "TL2", "vF", "d16", "q16", "bF", "th16", "room", "rest", "nrst", "a1", "a2", "t1", "uu", "act0", "w0", "ww", "hb", "ap",
+   "l1", "l2", "l3", "l4", "cnt4", "cum4", "gap4", "PF", "RI", "RM", "LM", "HU")
+sb(B2, 16, "kk", "kk2", "kq", "kq2")
+sb(H2, 16, "vS")
+sb(U2, 16, "vU", "topU", "bU", "qU", "vsU", "asU", "ovU", "dlU")
+sb(I4, 16, "IT", "IT2", "IT3")
+sb(I4, 16, "TPI")
+sb(B2, 48, "ilB", "CST")
+sb(F4, 48, "act3", "h3", "m3l", "p3", "topF")
+sb(U2, 48, "slU")
+sb(B2, 80, "FL", "SCM", "OV", "SC")
+sb(F4, 80, "CT", "P5", "q1", "q3")
+sb(B2, 576, "PK0", "PK1", "LD0", "LD1")
+SCRATCH["D"] = ("sbuf", [128, 16, 256], B2)
+SCRATCH["cT"] = ("sbuf", [128, 8, 32], H2)
+SCRATCH["HIL"] = ("sbuf", [1, 1024], B2)
+SCRATCH["THI"] = ("sbuf", [8, 256], I4)
+SCRATCH["TH8"] = ("sbuf", [8, 256], F4)
+SCRATCH["ZU"] = ("sbuf", [8, 144], F4)
+PSUM = ("pK", "pB", "pQ", "pL", "pE", "pN", "pX", "pC")
+for _b in PSUM[:7]:
+    SCRATCH[_b] = ("psum", [128, 512], F4)
+SCRATCH["pC"] = ("psum", [128, 16, 32], F4)
+SEMAPHORES = ["sv", "st", "ss", "sg", "ra0", "ra1", "rl"] + ["dm%d" % i for i in range(16)]
+
+
+def rank_program(g, core, T, topo):
+    rank = T.rank_of(core)
+    if rank is None:
+        return
+    nrank = len(T.cores)
+    Q = {"v": g.vector, "t": g.tensor, "s": g.scalar, "g": g, "y": g.sync}
+    SEM = {"v": "sv", "t": "st", "s": "ss", "g": "sg"}
+    count = {k: 0 for k in SEM.values()}
+    know = {q: {} for q in Q}
+    clocks = {}
+    acc = {}
+    ndma = [0]
+    prog = []
+    lab = [""]
+    group = []
+
+    def R(name, c0=0, c1=None, st=1, p=128):
+        buf, o, n = PART[name] if name in PART else (name, 0, SCRATCH[name][1][1])
+        if c1 is None:
+            c1 = n
+        t = T[buf]
+        return (name, t[0:p, o + c0:o + c1:st] if st > 1 else t[0:p, o + c0:o + c1], c0, c1, st)
+
+    def D3(c0, c1, k0=0, k1=256):
+        return ("D", T.D[:, c0:c1, k0:k1], 256 * c0, 256 * c1, 1)
+
+    def apart(a, b):
+        if a[1] >= b[2] or b[1] >= a[2]:
+            return True
+        return a[3] == b[3] and a[3] > 1 and (a[1] - b[1]) % a[3] != 0
+
+    def order(q, reads, writes):
+        need = {}
+        for is_w, lst in ((False, reads), (True, writes)):
+            for (name, _, c0, c1, st) in lst:
+                me = (is_w, c0, c1, st)
+                for rec_ in acc.get(name, ()):
+                    if name in PSUM:
+                        if rec_[6] == q and (q == "t" or not (is_w or rec_[0]) or apart(me, rec_)):
+                            continue
+                    elif not (is_w or rec_[0]) or apart(me, rec_):
+                        continue
+                    if know[q].get(rec_[4], 0) < rec_[5]:
+                        need[rec_[4]] = max(need.get(rec_[4], 0), rec_[5])
+        for s in list(need):
+            for o in list(need):
+                if o != s and need[s] and clocks[(s, need[s])].get(o, 0) >= need.get(o, 0):
+                    need[o] = 0
+        for s, n in need.items():
+            if n:
+                Q[q].wait_ge(T.sem[s], n)
+                for k, x in clocks[(s, n)].items():
+                    know[q][k] = max(know[q].get(k, 0), x)
+                know[q][s] = max(know[q].get(s, 0), n)
+
+    def note(q, sem, n, reads, writes):
+        clocks[(sem, n)] = dict(know[q])
+        for is_w, lst in ((False, reads), (True, writes)):
+            for (name, _, c0, c1, st) in lst:
+                old = acc.get(name, [])
+                if is_w:
+                    old = [r for r in old if not (c0 <= r[1] and r[2] <= c1 and st == 1 and (name not in PSUM or r[6] == q))]
+                else:
+                    old = [r for r in old if not (not r[0] and r[6] == q and c0 <= r[1] and r[2] <= c1 and st == 1)]
+                old.append((is_w, c0, c1, st, sem, n, q))
+                acc[name] = old
+
+    def rec(q, run, writes, reads, cost, lat=0.0):
+        prog.append((q, run, reads, writes, cost, lat, PRI.get(lab[0], 0.0)))
+
+    def nel(o):
+        if o[0] == "ind":
+            return 16 * (o[2][3] - o[2][2])
+        return (o[3] - o[2] + o[4] - 1) // o[4]
+
+    def small(o):
+        return o[0] != "ind" and info(o[0])[0] == "sbuf" and info(o[0])[2] in (B2, H2, U2)
+
+    def vcost(out, ins, full):
+        if out[0] == "ind":
+            return 60.0 + 4.0 * nel(out)
+        for o in ins:
+            if o[0] == "ind":
+                return 60.0 + 1.6 * nel(o)
+        if full:
+            return max(66.0, (2.07 if all(info(o[0])[0] == "sbuf" for o in ins) else 1.04) * nel(out))
+        return max(66.0, (0.52 if all(small(o) for o in list(ins) + [out]) else 1.04) * nel(out))
+
+    def flush():
+        n = len(prog)
+        preds = [{} for _ in range(n)]
+        hist = {}
+        for i, (q, run, reads, writes, cost, lat, pri) in enumerate(prog):
+            for is_w, lst in ((False, reads), (True, writes)):
+                for (name, _, c0, c1, st) in lst:
+                    me = (is_w, c0, c1, st)
+                    for r in hist.get(name, ()):
+                        far = apart(me, r)
+                        if name in PSUM:
+                            hit = (q != r[4]) or (not far and (is_w or r[0]))
+                        else:
+                            hit = not far and (is_w or r[0])
+                        if hit and r[5] != i:
+                            preds[i][r[5]] = True
+            for is_w, lst in ((False, reads), (True, writes)):
+                for (name, _, c0, c1, st) in lst:
+                    old = hist.get(name, [])
+                    if is_w:
+                        old = [r for r in old if not (c0 <= r[1] and r[2] <= c1 and st == 1 and (name not in PSUM or r[4] == q))]
+                    old.append((is_w, c0, c1, st, q, i))
+                    hist[name] = old
+        succ = [[] for _ in range(n)]
+        for i in range(n):
+            for p in preds[i]:
+                succ[p].append(i)
+        tail = [0.0] * n
+        for i in range(n - 1, -1, -1):
+            tail[i] = prog[i][4] + prog[i][5] + max([tail[j] + (WAKE if prog[j][0] != prog[i][0] else 15.0) for j in succ[i]] + [0.0])
+        left = [len(p) for p in preds]
+        ready = {q: [] for q in Q}
+        for i in range(n):
+            if not left[i]:
+                ready[prog[i][0]].append((0.0, i))
+        free = {q: 0.0 for q in Q}
+        at = {}
+        seq = []
+        while len(seq) < n:
+            pick = None
+            for q in Q:
+                if ready[q]:
+                    t = max(free[q], min(r[0] for r in ready[q]))
+                    if pick is None or t < pick[0]:
+                        pick = (t, q)
+            t, q = pick
+            r = max([r for r in ready[q] if r[0] <= t + 1e-6], key=lambda z: tail[z[1]] + prog[z[1]][6])
+            ready[q].remove(r)
+            i = r[1]
+            free[q] = t + prog[i][4]
+            seq.append(i)
+            fin = t + prog[i][4] + prog[i][5]
+            for j in succ[i]:
+                at[j] = max(at.get(j, 0.0), fin + (WAKE if prog[j][0] != q else 15.0))
+                left[j] -= 1
+                if not left[j]:
+                    ready[prog[j][0]].append((at[j], j))
+        TOT[0] = max(free.values())
+        for i in seq:
+            q, run, reads, writes, cost, lat, pri = prog[i]
+            run(q, reads, writes)
+
+    def single(make):
+        def run(q, reads, writes):
+            order(q, reads, writes)
+            s = SEM[q]
+            for m in make:
+                count[s] += 1
+                m().then_inc(T.sem[s], 1)
+            note(q, s, count[s], reads, writes)
+        return run
+
+    def dma(q, out, in_, writes, reads):
+        s = "dm%d" % ndma[0]
+        ndma[0] += 1
+
+        def run(q_, rds, wrs):
+            order(q_, rds, wrs)
+            Q[q_].dma_start(out, in_).then_inc(T.sem[s], 16)
+            note(q_, s, 16, rds, wrs)
+        rec(q, run, writes, reads, 60.0, 2500.0)
+
+    def ind(win, off):
+        return ("ind", win, off)
+
+    def ap(o):
+        return o[1][1].indirect(o[2][1]) if o[0] == "ind" else o[1]
+
+    def rd(*os):
+        out = []
+        for o in os:
+            if isinstance(o, tuple):
+                out += [o[1], o[2]] if o[0] == "ind" else [o]
+        return out
+
+    def sc(x):
+        return x[1] if isinstance(x, tuple) else x
+
+    def emit(q, make, out, ins, cost):
+        i = out[0] == "ind"
+        rec(q, single([make]), [out[1]] if i else [out], rd(*ins) + ([out[2]] if i else []), cost)
+
+    def tt(out, a, b, op):
+        emit("v", lambda: g.vector.tensor_tensor(ap(out), ap(a), ap(b), op), out, (a, b), vcost(out, (a, b), True))
+
+    def ts(out, a, s1, op0, s2=None, op1=None):
+        c = vcost(out, (a,), False)
+        if op1 is None:
+            emit("v", lambda: g.vector.tensor_scalar(ap(out), ap(a), sc(s1), None, op0), out, (a, s1), c)
+        else:
+            emit("v", lambda: g.vector.tensor_scalar(ap(out), ap(a), sc(s1), sc(s2), op0, op1), out, (a, s1, s2), c)
+
+    def tc(out, a):
+        emit("v", lambda: g.vector.tensor_copy(ap(out), ap(a)), out, (a,), vcost(out, (a,), False))
+
+    def ms(out, x):
+        emit("v", lambda: g.vector.memset(ap(out), x), out, (), vcost(out, (), False))
+
+    def scan(out, d0, d1, init, op0, op1):
+        emit("v", lambda: g.vector.tensor_tensor_scan(ap(out), ap(d0), ap(d1), init, op0, op1), out, (d0, d1), vcost(out, (d0, d1), False))
+
+    def act(out, a, f, bias=0.0, scale=1.0):
+        emit("s", lambda: g.scalar.activation(ap(out), ap(a), f, bias=bias, scale=sc(scale)), out, (a, scale),
+             80.0 + max(64.0, (1.5 if a[0] == "ind" else 1.0) * nel(out)) * 1.04)
+
+    def mm(out, l, r, start, stop):
+        c = ((lambda: g.tensor.matmul(out[1], l[1], r[1], start, stop)), [l, r], out, max(64, nel(out)) * PEC * (4 if info(l[0])[2] == F4 else 1))
+        if group:
+            group[-1].append(c)
+        else:
+            rec("t", single([c[0]]), [out], [l, r], c[3])
+
+    def grp(fn, rds=None, wrs=None):
+        group.append([])
+        fn()
+        calls = group.pop()
+        reads, writes = [], []
+        for c in calls:
+            reads += [o for o in c[1] if o not in reads]
+            if c[2] not in writes:
+                writes.append(c[2])
+        rec("t", single([c[0] for c in calls]), wrs or writes, rds or reads, sum(c[3] for c in calls))
+
+    def mms(*calls):
+        def run():
+            for n, (o, l, r) in enumerate(calls):
+                mm(o, l, r, n == 0, n == len(calls) - 1)
+        grp(run)
+
+    def sel(out, in_, pat, op, base, cm, fill=0.0):
+        emit("g", lambda: g.affine_select(ap(out), ap(in_), pat, op, fill, base, cm), out, (in_,), 170.0 + 2.1 * nel(out))
+
+    def iota(out, pat, base, cm):
+        emit("g", lambda: g.iota(ap(out), pat, base, cm, allow_small_or_imprecise_dtypes=True), out, (), 130.0 + 2.1 * nel(out))
+
+    def lay(out, c0, src, z):
+        def run():
+            for r in range(16):
+                mm(R(out, c0, c0 + 16), R(z, 15 - r, 143 - r), R(src, r, 256, 16), r == 0, r == 15)
+        grp(run, [R(src, 0, 256), R(z)], [R(out, c0, c0 + 16)])
+
+    def spread(out, c0, w, src):
+        def run():
+            for r in range(16):
+                mm(R(out, c0 + r, c0 + 256, 16), R(w, 128 * r, 128 * r + 128), R(src, 0, 16), True, True)
+        grp(run, [R(w), R(src, 0, 16)], [R(out, c0, c0 + 256)])
+
+    def one(n, p=128):
+        return R("ONE", 0, n, 1, p)
+
+    def row(nm, a=0, b=256):
+        return R(nm, a, b, 1, 1)
+
+    dma("y", T.TPI[:], T.tops[:], [R("TPI")], [])
+    dma("s", T.X[:], T.x0[:], [R("X")], [])
+    dma("y", T.KI[:, 0:768], T.kids[:, 0:768], [R("KI", 0, 768)], [])
+    dma("s", T.A[:, 0:1536], T.a0[:], [R("A", 0, 1536)], [])
+    dma("y", T.KI[:, 768:1536], T.kids[:, 768:1536], [R("KI", 768, 1536)], [])
+    dma("y", T.THI[:], T.th[:], [R("THI", p=8)], [])
+    ms(R("ONE"), 1.0)
+    iota(R("IT"), [[0, 16]], 0, 1)
+    iota(R("IT2"), [[16, 16]], 0, 0)
+    iota(R("IT3"), [[0, 16]], 0, 1)
+    sel(R("BLK"), one(128), [[-16, 8], [0, 16]], OP.is_ge, 0, 1)
+    sel(R("BLK"), R("BLK"), [[16, 8], [0, 16]], OP.is_ge, 15, -1)
+    iota(R("RI"), [[1, 16]], 0, 0)
+    sel(R("Z1"), one(144), [[-16, 9], [0, 16]], OP.is_ge, 0, 1)
+    sel(R("Z1"), R("Z1"), [[16, 9], [0, 16]], OP.is_ge, 15, -1)
+    sel(R("Z1"), R("Z1"), [[0, 9], [1, 16]], OP.is_equal, -15, 0)
+    sel(R("ID"), one(128), [[-1, 128]], OP.is_equal, 0, 1)
+    iota(row("LOI"), [[0, 16], [2, 16]], -15, 0)
+    iota(R("KW"), [[0, 8], [512, 16]], -3840, 0)
+    sel(R("TA"), R("BLK"), [[1, 128]], OP.is_ge, -1, -1)
+    iota(row("tmpf"), [[1, 256]], 1, 0)
+    ms(R("RS"), -BIG)
+    sel(R("RS2"), R("RS"), [[0, 16], [1, 16]], OP.not_equal, -1, 0, BIG)
+    sel(R("RS"), R("RS"), [[0, 16], [1, 16]], OP.not_equal, 0, 0, BIG)
+    iota(R("NB0"), [[1, 256]], -511, 0)
+    ms(R("ZU", p=8), 1.0)
+    sel(R("ZU", p=8), R("ZU", p=8), [[1, 144]], OP.is_equal, -15, -16)
+    sel(R("SCM"), one(80), [[0, 5], [1, 16]], OP.not_equal, 0, 0)
+    sel(R("TN"), R("BLK"), [[-1, 128]], OP.is_ge, 0, 1)
+    ms(R("A", 1536, 3840), 0.0)
+    ms(R("A", 3840, 4096), 8192.0)
+    ts(R("IT"), R("IT"), 15, OP.bitwise_and)
+    tt(R("il"), R("IT"), R("IT2"), OP.add)
+    tc(R("PF"), R("IT"))
+    ts(R("IT3"), R("IT3"), 16, OP.bitwise_and)
+    tc(R("HU", 1, 2), R("IT3", 0, 1))
+    ts(R("HU", 1, 2), R("HU", 1, 2), 0.0625, OP.mult)
+    ts(R("HU", 0, 1), R("HU", 1, 2), -1.0, OP.mult, 1.0, OP.add)
+    tc(R("topU"), R("TPI"))
+    tc(R("topF", 0, 16), R("TPI"))
+
+    def newx():
+        for k in range(16):
+            o = R("X16", k, 4096, 16)
+            if k % 3 == 2:
+                act(o, R("X"), AF.Copy)
+            else:
+                tc(o, R("X"))
+        act(R("CA", 256, 512), R("X"), AF.Copy)
+
+    newx()
+    ts(R("RM"), R("RI"), R("PF", 0, 1), OP.is_equal)
+    for u in range(2):
+        for w in range(2):
+            nm = "S%d%d" % (u, w)
+            sel(R(nm), R("ID") if u == w else one(128), [[-1, 128]], OP.is_equal, 16 * (w - u), 1)
+            ts(R(nm), R(nm), R("HU", u, u + 1), OP.mult)
+    ts(R("LM"), R("RI"), R("PF", 0, 1), OP.is_gt)
+    act(R("C", 1536, 3584), R("ONE"), AF.Identity, 4095.0, 0.0)
+    act(R("C", 3584, 4096), one(512), AF.Identity, 4095.0, 0.0)
+    ts(R("Z16"), R("Z1"), 16.0, OP.mult)
+    tt(R("KW"), R("KW"), R("BLK"), OP.mult)
+    ts(row("KC"), row("LOI"), 0.5, OP.mult)
+    tt(row("CK", 0, 128), row("LOI", 0, 128), row("LOI", 0, 128), OP.mult)
+    ts(row("CK", 0, 128), row("CK", 0, 128), -64.0, OP.mult, 128.0, OP.add)
+    for nm, x in (("IN", -1.0), ("IN256", -256.0)):
+        ts(R(nm), R("ID"), x, OP.mult)
+    ts(R("TA"), R("TA"), 512.0, OP.mult)
+    tt(R("T2"), R("TA"), R("IN256"), OP.add)
+    ts(row("LOI"), row("tmpf"), 0.0625, OP.mult)
+    ms(R("HIL", 0, 128, 1, 1), 224.0)
+    ms(row("CMH", 0, 128), -0.5)
+    tc(R("C", 0, 768), R("KI", 0, 768))
+    tc(R("C", 768, 1536), R("KI", 768, 1536))
+
+    def setup2():
+        for r in range(16):
+            act(R("BA", 128 * r, 128 * r + 128), R("KW"), AF.Copy, 0.0, R("RM", r, r + 1))
+        for r in range(16):
+            ts(R("BC", 128 * r, 128 * r + 128), R("BLK"), R("RM", r, r + 1), OP.mult)
+        ts(R("BB"), R("BC"), -256.0, OP.mult)
+        for nm, x in (("IN2", -2.0), ("I4K", 4096.0), ("IN128", -128.0), ("IN16", -0.0625), ("I512", 512.0), ("IN512", -512.0)):
+            ts(R(nm), R("ID"), x, OP.mult)
+
+    def setup3():
+        for r in range(16):
+            ts(R("TB", 128 * r, 128 * r + 128), R("BLK"), R("LM", r, r + 1), OP.mult)
+        ts(R("NB0"), R("NB0"), 0.0625, OP.mult)
+        ts(R("TN"), R("TN"), -1.0, OP.mult)
+        for j in range(3):
+            tc(R("ilB", 16 * j, 16 * j + 16), R("il"))
+            ms(R("CST", 16 * j, 16 * j + 16), (0.0, 512.0, 256.0)[j])
+        ms(R("ww"), 1.0)
+        ts(R("TR"), R("il"), 3584.0, OP.add)
+        ts(R("TL2"), R("il"), 320.0, OP.add)
+        for t in range(4):
+            ts(R("CT", 16 * t, 16 * t + 16), R("il"), -1.0, OP.mult, 80.0 * t - 320.0, OP.add)
+        ms(row("CM128", 0, 128), 128.0)
+        for s in range(1, 8):
+            ms(R("HIL", 128 * s, 128 * s + 128, 1, 1), 224.0 + 16.0 * s)
+        ms(R("CA", 512, 768), 0.0)
+        ms(R("CN", 256, 512), 0.0)
+        ms(R("PK0"), 0.0)
+        ms(R("PK1"), 0.0)
+        tc(R("TH8", p=8), R("THI", p=8))
+        mms(*[(R("pL", 0, 16), R("ZU", 15 - r, 143 - r, 1, 8), R("TH8", r, 256, 16, 8)) for r in range(16)])
+        ts(R("th16"), R("pL", 0, 16), 16.0, OP.mult)
+
+    MID = ("pC", T.pC[:, 8:16, :], 256, 512, 1)
+    CT3 = ("cT", T.cT[:], 0, 256, 1)
+    AW, CW = R("A"), R("C")
+
+    def pairs_front():
+        ts(R("vBU"), R("pN", 0, 256), 2048.0, OP.add)
+        for c in range(16):
+            ts(R("IND", 272 * c, 256 * c + 256), R("vBU", 16 * c, 256), R("vF", c, c + 1), OP.is_equal, R("ww", c, c + 1), OP.mult)
+
+    def pairs_count():
+        def run():
+            mm(R("pX", 256, 512), R("TB", 0, 128), R("IND", 0, 256), True, False)
+            for c in range(15):
+                mm(R("pX", 256 + 16 * (c + 1), 512), R("BLK"), R("IND", 272 * c + 16, 256 * c + 256), False, False)
+            for r in range(1, 16):
+                mm(R("pX", 256 + r, 512, 16), R("TB", 128 * r, 128 * r + 128), R("IND", r, 4096, 272), False, r == 15)
+        grp(run, [R("IND"), R("TB"), R("BLK")], [R("pX", 256, 512)])
+
+    def pairs_list():
+        act(R("CNM"), R("pX", 256, 512), AF.Copy)
+        lay("pL", 64, "CNM", "Z1")
+
+    def set_act(src):
+        for j in range(3):
+            act(R("act3", 16 * j, 16 * j + 16), src, AF.Copy)
+        act(R("FL", 0, 16), src, AF.Copy)
+
+    def keys(ph, c0, c1):
+        o = R("pK", 256 + 16 * c0, 256 + 16 * c1) if ph == 2 else R("pK", 16 * c0, 16 * c1) if c0 < 8 else R("pB", 256 + 16 * c0, 256 + 16 * c1)
+
+        def run():
+            if ph == 1:
+                mm(o, R("ONE", 0, 128, 1, 1), row("KC", 16 * c0, 16 * c1), True, False)
+            for r in range(16):
+                mm(o, R("Z16", 15 - r, 143 - r), D3(c0, c1, 16 * r, 16 * r + 16), ph == 2 and r == 0, r == 15)
+        grp(run, [D3(c0, c1), R("Z16")] + ([R("ONE"), row("KC")] if ph == 1 else []), [o])
+
+    def vdiff(ph, lst, a, b):
+        lab[0] = "v%d%d" % (ph, a // 8)
+        tt(R("E", 256 * a, 256 * b), ind(AW, R(lst, 16 * a, 16 * b)), R("X16", 256 * a, 256 * b), OP.subtract)
+        lab[0] = ""
+
+    def vabs(ph, a, b):
+        act(D3(a, b), R("E", 256 * a, 256 * b), AF.Abs)
+        keys(ph, a, b)
+
+    def sgather(lst, a, b):
+        n = 256 * (b - a)
+        act(R("G", 0, n), ind(AW, R(lst, 16 * a, 16 * b)), AF.Copy)
+        mms((R("pX", 0, n), R("ID"), R("G", 0, n)), (R("pX", 0, n), R("IN"), R("X16", 256 * a, 256 * b)))
+
+    def sabs(ph, a, b):
+        act(D3(a, b), R("pX", 0, 256 * (b - a)), AF.Abs)
+        keys(ph, a, b)
+
+    def onehot(bank, k1, k2, h):
+        def run():
+            mm(R(bank, 128 * h, 128 * h + 128), row("CK", 0, 128), one(128, 1), True, False)
+            for w, src, last in (("BA", k1, False), ("BB", k2, True)):
+                for r in range(16):
+                    mm(R(bank, 128 * h + r, 128 * h + 128, 16), R(w, 128 * r, 128 * r + 128), R(src, 8 * h, 8 * h + 8), False, last and r == 15)
+        grp(run, [row("CK", 0, 128), R("BA"), R("BB"), R(k1, 8 * h, 8 * h + 8), R(k2, 8 * h, 8 * h + 8)], [R(bank, 128 * h, 128 * h + 128)])
+
+    def hlay(c0, src, k2, h):
+        o = R("pL", c0 + 8 * h, c0 + 8 * h + 8)
+
+        def run():
+            for r in range(16):
+                mm(o, R("Z1", 15 - r, 143 - r), R(src, 128 * h + r, 128 * h + 128, 16), r == 0, False)
+            mm(o, R("I4K"), R(k2, 8 * h, 8 * h + 8), False, True)
+        grp(run, [R(src, 128 * h, 128 * h + 128), R("Z1"), R("I4K"), R(k2, 8 * h, 8 * h + 8)], [o])
+
+    def kh(h, o=0):
+        return R("pB", 384 + o, 512) if h else R("pK", o, 128)
+
+    def split16(m, off, dd, kk, kk2, h):
+        src = R(m, 128 * h + off, 128 * h + (128 if off == 15 else 127), 16)
+        e = (8 * h, 8 * h + 8)
+        ts(R(dd, *e), src, 201326592.0, OP.add, -201326592.0, OP.add)
+        tt(R(kk, *e), src, R(dd, *e), OP.subtract)
+        act(R(kk2, *e), R(kk, *e), AF.Square)
+
+    def best(h):
+        lab[0] = "best"
+        w = (128 * h, 128 * h + 128)
+        e = (8 * h, 8 * h + 8)
+        scan(R("m1", *w), R("RS", *w), kh(h), BIG, OP.max, OP.min)
+        tt(R("nB", *w), kh(h), R("m1", *w), OP.is_equal)
+        tt(R("zz", 128 * h + 1, 128 * h + 128), kh(h, 1), R("m1", 128 * h, 128 * h + 127), OP.max)
+        ts(R("nN", *w), R("nB", *w), -1.0, OP.mult, 1.0, OP.add)
+        tt(R("yB", *w), R("nB", *w), ("pC", T.pC[:, 4 * h:4 * h + 4, :], 128 * h, 128 * h + 128, 1), OP.mult)
+        scan(R("sB", *w), R("nN", *w), R("yB", *w), 0.0, OP.mult, OP.add)
+        ts(R("bU", *e), R("sB", 128 * h + 15, 128 * h + 128, 16), 2047.0, OP.add)
+        ts(R("bF", *e), R("sB", 128 * h + 15, 128 * h + 128, 16), 2047.0, OP.add)
+        split16("m1", 15, "d16", "kk", "kk2", h)
+        onehot("pB", "kk", "kk2", h)
+        lab[0] = ""
+
+    def second(h):
+        lab[0] = "sec"
+        a, b = 128 * h, 128 * h + 128
+        scan(R("m2", a, b - 1), R("RS2", 1, 128), R("zz", a + 1, b), BIG, OP.max, OP.min)
+        split16("m2", 14, "q16", "kq", "kq2", h)
+        lab[0] = "oq"
+        onehot("pQ", "kq", "kq2", h)
+        lab[0] = ""
+
+    def bgather(h):
+        lab[0] = "bg"
+        tc(R("dU", 128 * h, 128 * h + 128), ind(CW, R("bU", 8 * h, 8 * h + 8)))
+        lab[0] = ""
+
+    def sgath(h):
+        lab[0] = "sg"
+        w, e = (128 * h, 128 * h + 128), (8 * h, 8 * h + 8)
+        act(R("AB", *w), ind(AW, R("bU", *e)), AF.Copy)
+        act(R("dtf", *w), ind(CW, R("bU", *e)), AF.Identity, -127.9375, 0.0625)
+        lab[0] = ""
+
+    def qlist(h):
+        lab[0] = "ql"
+        w, e = (128 * h, 128 * h + 128), (8 * h, 8 * h + 8)
+        tt(R("ZQ", *w), R("pQ", *w), R("ct", *w), OP.min)
+        hlay(16, "ZQ", "kq2", h)
+        ts(R("qU", *e), R("pL", 16 + 8 * h, 24 + 8 * h), 16.0, OP.mult, 1363967.0, OP.add)
+        lab[0] = ""
+
+    def transp():
+        return g.vector.transpose(T.cT[:], T.cH[:])
+
+    def children(lst):
+        tc(R("cU"), ind(CW, R(lst)))
+        ts(R("cH"), R("cU"), -2047.0, OP.add)
+        emit("v", transp, CT3, (R("cH"),), 136.0)
+
+        def run():
+            for u in range(2):
+                for w in range(2):
+                    mm(("pC", T.pC[:, 0:8, 16 * u:16 * u + 16], 0, 128, 1), R("S%d%d" % (u, w)), ("cT", T.cT[:, :, 16 * w:16 * w + 16], 0, 256, 1), w == 0, w == 1)
+        grp(run, [CT3, R("S00"), R("S01"), R("S10"), R("S11")], [("pC", T.pC[:, 0:8, :], 0, 256, 1)])
+        lab[0] = "ch2"
+        act(R("ct"), ind(CW, R(lst)), AF.Identity, -127.9375, 0.0625)
+        act(R("EM"), R("ct"), AF.Relu, -2047.0, 16.0)
+        lab[0] = ""
+
+    def step(s):
+        t = s % 4
+        n0 = 1536 + 256 * s
+        vdiff(1, "cU", 0, 4)
+        sgather("cU", 14, 16)
+        vdiff(1, "cU", 4, 6)
+        vabs(1, 0, 4)
+        if s == 0:
+            setup2()
+        sabs(1, 14, 16)
+        vabs(1, 4, 6)
+        sgather("cU", 6, 8)
+        sabs(1, 6, 8)
+        vdiff(1, "cU", 8, 12)
+        best(0)
+        vdiff(1, "cU", 12, 14)
+        vabs(1, 8, 12)
+        vabs(1, 12, 14)
+        if s == 0:
+            setup3()
+        act(R("NBS"), R("NB0"), AF.Identity, 16.0 * s, 1.0)
+        pn = R("pN", 0, 256)
+        mms((pn, R("T2"), R("EM")), (pn, one(128, 1), row("LOI")), (pn, R("HIL", 128 * s, 128 * s + 128, 1, 1), one(256, 1)))
+        lay("pE", 16, "EM", "Z1")
+        second(0)
+        bgather(0)
+        best(1)
+        vdiff(2, "dU", 0, 4)
+        sgather("dU", 6, 8)
+        tt(R("CC", 256, 512), pn, R("ct"), OP.min)
+        ts(R("room"), R("pE", 16, 32), 0.0, OP.is_gt)
+        second(1)
+        bgather(1)
+        vdiff(2, "dU", 4, 6)
+        vabs(2, 0, 4)
+        sabs(2, 6, 8)
+        sgath(0)
+        vabs(2, 4, 6)
+        vdiff(2, "dU", 8, 12)
+        qlist(0)
+        qlist(1)
+        if s == 0:
+            spread("pN", 0, "BC", "vS")
+            pairs_front()
+            pairs_count()
+            pairs_list()
+            ts(R("act0"), R("pL", 64, 80), 0.0, OP.is_equal)
+            set_act(R("act0"))
+        vabs(2, 8, 12)
+        sgath(1)
+        lab[0] = "em"
+        act(R("AQ"), ind(AW, R("qU")), AF.Copy)
+        mms((MID, R("ID"), R("AB")), (MID, R("ID"), R("AQ")), (MID, row("CMH", 0, 128), one(256, 1)))
+        lab[0] = ""
+        tt(R("c2"), R("ct"), R("pB", 0, 256), OP.max)
+        vdiff(2, "dU", 12, 16)
+        tt(R("pB", 256, 512), R("pB", 0, 256), R("NBS"), OP.min)
+        tt(R("yy"), R("pQ", 0, 256), R("ct"), OP.max)
+        tt(R("CC", 0, 256), R("pB", 256, 512), R("yy"), OP.max)
+        act(R("SBN"), R("pB", 0, 256), AF.Sign, 0.0, -1.0)
+        act(R("SQN"), R("pQ", 0, 256), AF.Sign, 0.0, -1.0)
+        act(R("pE", 256, 512), R("c2"), AF.Identity, 524160.0, -4096.0)
+        vabs(2, 12, 16)
+        lab[0] = "em"
+        ts(R("M2"), MID, 25165824.0, OP.add, -25165824.0, OP.add)
+        mms((MID, R("ID"), R("M2")), (MID, R("IN2"), R("X")))
+        act(R("AM"), MID, AF.Abs, 0.0, 0.5)
+        lay("pL", 32, "AM", "Z16")
+        lab[0] = ""
+        px = R("pX", 256, 512)
+        mms((px, R("ID"), R("X")), (px, R("IN"), R("AB")))
+        ts(R("CLP"), px, -4.0, OP.max, 4.0, OP.min)
+        pg = R("pN", 256, 512)
+        mms((pg, R("IN128"), R("SBN")), (pg, R("IN128"), R("SQN")), (pg, R("IN16"), R("cH")), (pg, row("CM128", 0, 128), one(256, 1)))
+        tt(R("pE", 256, 512), R("pE", 256, 512), R("dtf"), OP.max)
+        tt(R("CC", 512, 768), R("pE", 256, 512), R("c2"), OP.min)
+        act(R("CN", 0, 256), pg, AF.Relu)
+        tt(R("m3l", 0, 16), R("vF"), R("TR"), OP.subtract)
+        ts(R("m3l", 32, 48), R("m3l", 0, 16), -1.0, OP.mult, float(n0 - 3584), OP.add)
+        ts(R("nF"), R("il"), float(n0), OP.add)
+        tt(R("m3l", 16, 32), R("bF"), R("nF"), OP.subtract)
+        tt(R("vact"), R("m3l", 0, 16), R("act3", 0, 16), OP.mult)
+        tt(R("vact"), R("vact"), R("TR"), OP.add)
+        tt(R("hb"), R("bF"), R("TR"), OP.subtract)
+        tt(R("a2"), R("pL", 32, 48), R("d16"), OP.min)
+        scan(R("m3"), R("RS"), R("pK", 256, 512), BIG, OP.max, OP.min)
+        es = R("m3", 15, 256, 16)
+        tt(R("a1"), es, R("th16"), OP.min)
+        tt(R("uu"), R("a2"), es, OP.min)
+        tt(R("t1"), R("pL", 32, 48), R("a1"), OP.min)
+        tt(R("h3", 16, 32), R("a2"), R("a1"), OP.is_le)
+        tt(R("h3", 32, 48), R("th16"), R("uu"), OP.is_lt)
+        tt(R("h3", 0, 16), R("d16"), R("t1"), OP.is_le)
+        tt(R("FL", 16, 64), R("h3"), R("act3"), OP.mult)
+        actB, hostA, hmA, newA, nrA = [R("FL", 16 * j, 16 * j + 16) for j in range(5)]
+        tt(R("p3", 16, 48), R("FL", 16, 48), R("m3l", 16, 48), OP.mult)
+        tt(R("vF"), R("vF"), R("p3", 16, 32), OP.add)
+        tt(R("vF"), R("vF"), R("p3", 32, 48), OP.add)
+        ts(R("vS"), R("vF"), -2048.0, OP.add)
+        tt(nrA, newA, R("room"), OP.mult)
+        spread("pN", 0, "BC", "vS")
+        o = R("pE", 64, 112)
+        o0, o1, o2 = R("pE", 64, 80), R("pE", 80, 96), R("pE", 96, 112)
+        mms((o, R("ID"), R("ilB")), (o, R("ID"), R("CST")), (o0, R("I512"), actB), (o0, R("IN512"), hmA), (o0, R("IN256"), newA), (o1, R("IN512"), hmA),
+            (o1, R("I512"), hostA), (o1, R("IN256"), nrA), (o2, R("IN256"), hmA), (o2, R("I512"), hostA), (o2, R("IN256"), hostA))
+        tt(R("nrst"), R("nrst"), newA, OP.subtract)
+        ts(R("w0"), hostA, 255.0, OP.mult)
+        tt(R("ww"), R("nrst"), R("w0"), OP.add)
+        tt(R("p3", 0, 16), hostA, R("m3l", 0, 16), OP.mult)
+        tt(R("p3", 0, 16), R("vact"), R("p3", 0, 16), OP.subtract)
+        tc(R("vsU"), R("p3", 0, 16))
+        pairs_front()
+        lab[0] = "sl"
+        tc(R("slU"), o)
+        act(R("selc"), ind(R("CC"), R("slU", 0, 16)), AF.Copy)
+        lab[0] = ""
+        act(R("C", n0, n0 + 256), ind(R("CN"), R("slU", 32, 48)), AF.Identity, 4095.0, -16.0)
+        act(R("CA", 0, 256), R("M2"), AF.Copy, 0.0, 0.5)
+        act(R("A", n0, n0 + 256), ind(R("CA"), R("slU", 16, 32)), AF.Copy)
+        pairs_count()
+        tc(R("vU"), R("vF"))
+        tt(R("hb"), R("hb"), hostA, OP.mult)
+        ts(ind(CW, R("vsU")), R("selc"), 16.0, OP.mult, 2047.0, OP.add)
+        lab[0] = "pl"
+        pairs_list()
+        lab[0] = ""
+        if s < 7:
+            children("vU" if t < 3 else "topU")
+        ts(R("ap"), R("pL", 64, 80), 4096.0, OP.is_lt)
+        tt(R("ap"), R("ap"), R("hb"), OP.mult)
+        tt(R("ap"), R("ap"), R("TR"), OP.add)
+        tc(R("asU"), R("ap"))
+        tt(ind(AW, R("asU")), R("AB"), R("CLP"), OP.add)
+        tt(R("OV", 16 * t, 16 * t + 16), newA, nrA, OP.subtract)
+        if t < 3:
+            ts(R("w0"), R("pL", 64, 80), 0.0, OP.is_equal)
+            tt(R("w0"), R("w0"), R("nrst"), OP.mult)
+            set_act(R("w0"))
+
+    def round_end(p):
+        PK, LD = "PK%d" % p, "LD%d" % p
+        ts(R("rest"), R("nrst"), -1.0, OP.mult, 1.0, OP.add)
+        tc(R("OV", 64, 80), R("rest"))
+        scan(R("SC"), R("SCM"), R("OV"), 0.0, OP.mult, OP.add)
+        mms((R("pX", 0, 80), R("BLK"), R("SC")), (R("pX", 0, 80), R("TN"), R("OV")))
+        mm(R("pX", 80, 84), R("BLK"), R("SC", 15, 64, 16), True, True)
+        tc(R("P5"), R("pX", 0, 80))
+        ts(R("q1", 0, 64), R("P5", 0, 64), 64.0, OP.is_lt)
+        tt(R("q1", 0, 64), R("q1", 0, 64), R("OV", 0, 64), OP.mult)
+        tt(R("q3", 0, 64), R("P5", 0, 64), R("CT", 0, 64), OP.add)
+        tt(R("q3", 0, 64), R("q3", 0, 64), R("q1", 0, 64), OP.mult)
+        tt(R("q1", 0, 32), R("q3", 0, 32), R("q3", 32, 64), OP.add)
+        tt(R("l1"), R("q1", 0, 16), R("q1", 16, 32), OP.add)
+        tt(R("l1"), R("l1"), R("TL2"), OP.add)
+        tc(R("ovU"), R("l1"))
+        tc(ind(R(PK), R("ovU")), R("X"))
+        ts(R(PK, 64, 320, 80), R("pX", 80, 84), 64.0, OP.min)
+        tr = []
+        for t in range(4):
+            dst = T.cores[(rank + 1 + (4 * p + t) % (nrank - 1)) % nrank]
+            e = topo.engines(core, dst)
+            rid, pid, _ = topo.addr(dst)
+            tr.append(RemoteDMATransfer(dst_ids=[DstId(rid=rid, pnc=pid)], dma_engine_mask=(1 << e[2 * t]) | (1 << e[2 * t + 1]), remote_sem=T.sem["ra%d" % p],
+                                        srcs=[T[PK][:, 80 * t:80 * t + 80]], dsts=[T[LD][:, 80 * t:80 * t + 80]]))
+
+        def send(q, reads, writes):
+            order(q, reads, [])
+            g.remote_dma_fused(tr, local_sem=T.sem.rl)
+            clocks[("ra%d" % p, 8)] = {}
+            acc.setdefault(LD, []).append((True, 0, 320, 1, "ra%d" % p, 8, "remote"))
+        rec("g", send, [R(LD, 0, 320)], [R(PK, 0, 320)], 1500.0, 2500.0)
+        act(R("AV"), ind(AW, R("vU")), AF.Copy)
+        pn = R("pN", 0, 256)
+        mms((pn, R("ID"), R("X")), (pn, R("IN"), R("AV")))
+        act(R(LD, 320, 576), pn, AF.Abs)
+        tc(R("cnt4", 0, 4), R(LD, 64, 320, 80))
+        scan(R("cum4", 0, 4), one(4), R("cnt4", 0, 4), 0.0, OP.mult, OP.add)
+        ts(R("gap4", 0, 4), R("cnt4", 0, 4), -1.0, OP.mult, 80.0, OP.add)
+        nr = R("P5", 64, 80)
+        for j in range(3):
+            ts(R("l%d" % (j + 1)), nr, R("cum4", j, j + 1), OP.is_ge, R("gap4", j, j + 1), OP.mult)
+        ts(R("l4"), nr, R("cum4", 3, 4), OP.is_lt)
+        tt(R("l1"), R("l1"), R("l2"), OP.add)
+        tt(R("l3"), R("l3"), nr, OP.add)
+        tt(R("l1"), R("l1"), R("l3"), OP.add)
+        tt(R("l4"), R("l4"), R("rest"), OP.mult)
+        tt(R("l1"), R("l1"), R("TL2"), OP.subtract)
+        tt(R("l1"), R("l1"), R("l4"), OP.mult)
+        tt(R("l1"), R("l1"), R("TL2"), OP.add)
+        tc(R("dlU"), R("l1"))
+        tc(R("X"), ind(R(LD), R("dlU")))
+
+    tc(R("vU"), R("topU"))
+    tc(R("vF"), R("topF", 0, 16))
+    ts(R("vS"), R("vF"), -2048.0, OP.add)
+    children("topU")
+    for p in range(2):
+        if p:
+            newx()
+            tc(R("vU"), R("topU"))
+            tc(R("vF"), R("topF", 0, 16))
+            set_act(R("act0"))
+        ms(R("nrst"), 1.0)
+        for t in range(4):
+            step(4 * p + t)
+        if p:
+            dma("y", T.yc[:], T.C[:, 0:3584], [], [R("C", 0, 3584)])
+            dma("y", T.ya[:], T.A[:, 0:3584], [], [R("A", 0, 3584)])
+        round_end(p)
+    dma("y", T.yx[:], T.X[:], [], [R("X")])
+    flush()
+    g.wait_ge(T.sem.rl, 16)
+    for i in range(6, ndma[0]):
+        g.sync.wait_ge(T.sem["dm%d" % i], 16)
+    for q in ("v", "t", "s", "g"):
+        g.sync.wait_ge(T.sem[SEM[q]], count[SEM[q]])

@@ -5,7 +5,8 @@ AF = ActivationFunctionType
 B2, F4, H2, I4, U2 = "bfloat16", "float32", "float16", "int32", "uint16"
 BIG = 1.0e9
 PEC, WAKE = 0.52, 75.0
-PRI = {"sl": 1500, "em": 3000, "ql": 6000, "bg": 3000, "sg": -1500, "v21": -1500, "v20": 1500}
+PRI = {"re": 30000, "sl": 20000, "em": 3000, "ql": 6000, "bg": 3000, "sg": -1500, "v21": -1500, "v20": -1500, "v11": -3000, "oq": 20000, "v10": -3000, "sec": -1500,
+       "sp": 20000, "cn": -3000}
 TOT = [0.0]
 SCRATCH = {}
 
@@ -35,23 +36,26 @@ sb(B2, 2048, "ONE", "BC", "BA", "BB", "TB")
 sb(B2, 128, "BLK", "ID", "IN", "IN2", "I4K", "IN128", "IN16", "I512", "IN512", "IN256", "TN", "T2", "TA", "CK", "CM128", "CMH", "KW", "S00", "S01", "S10", "S11")
 sb(B2, 144, "Z1", "Z16")
 sb(B2, 256, "X")
-sb(B2, 256, "KC", "LOI", "EM", "M2", "AM", "AB", "CLP", "SBN", "SQN", "CNM", "AV", "AQ", "nB", "nN")
-sb(F4, 256, "NB0", "NBS", "RS", "RS2", "ct", "dtf", "m1", "m2", "m3", "zz", "c2", "yy", "selc", "tmpf", "yB", "sB")
+sb(B2, 256, "KC", "LOI", "EM", "M2", "AM", "AB", "CLP", "CNM", "AV", "AQ", "nB", "nN")
+sb(F4, 256, "NB0", "RS", "RS2", "ct", "dtf", "m1", "m2", "m3", "zz", "c2", "yy", "selc", "tmpf", "yB", "sB")
 sb(H2, 256, "ZQ", "cH")
 sb(U2, 256, "cU", "dU", "vBU")
 sb(I4, 1536, "KI")
 sb(F4, 768, "CC")
+sb(F4, 2048, "NB8")
+sb(F4, 128, "NF8")
+sb(B2, 512, "SGN")
 sb(F4, 512, "CN")
 sb(B2, 768, "CA")
-sb(F4, 16, "il", "nF", "vact", "TR", "TL2", "vF", "d16", "q16", "bF", "th16", "room", "rest", "nrst", "a1", "a2", "t1", "uu", "act0", "w0", "ww", "hb", "ap",
+sb(F4, 16, "il", "TRB", "vact", "TR", "TL2", "vF", "d16", "q16", "th16", "rest", "nrst", "a1", "a2", "t1", "uu", "act0", "w0", "ww", "hb", "ap",
    "l1", "l2", "l3", "l4", "cnt4", "cum4", "gap4", "PF", "RI", "RM", "LM", "HU")
-sb(B2, 16, "kk", "kk2", "kq", "kq2")
+sb(B2, 32, "KK", "KK2")
 sb(H2, 16, "vS")
 sb(U2, 16, "vU", "topU", "bU", "qU", "vsU", "asU", "ovU", "dlU")
 sb(I4, 16, "IT", "IT2", "IT3")
 sb(I4, 16, "TPI")
 sb(B2, 48, "ilB", "CST")
-sb(F4, 48, "act3", "h3", "m3l", "p3", "topF")
+sb(F4, 48, "h3", "m3l", "p3", "topF")
 sb(U2, 48, "slU")
 sb(B2, 80, "FL", "SCM", "OV", "SC")
 sb(F4, 80, "CT", "P5", "q1", "q3")
@@ -229,7 +233,7 @@ def rank_program(g, core, T, topo):
             note(q, s, count[s], reads, writes)
         return run
 
-    def dma(q, out, in_, writes, reads):
+    def dma(q, out, in_, writes, reads, lat=2500.0):
         s = "dm%d" % ndma[0]
         ndma[0] += 1
 
@@ -237,7 +241,7 @@ def rank_program(g, core, T, topo):
             order(q_, rds, wrs)
             Q[q_].dma_start(out, in_).then_inc(T.sem[s], 16)
             note(q_, s, 16, rds, wrs)
-        rec(q, run, writes, reads, 60.0, 2500.0)
+        rec(q, run, writes, reads, 60.0, lat)
 
     def ind(win, off):
         return ("ind", win, off)
@@ -417,7 +421,8 @@ def rank_program(g, core, T, topo):
     def setup3():
         for r in range(16):
             ts(R("TB", 128 * r, 128 * r + 128), R("BLK"), R("LM", r, r + 1), OP.mult)
-        ts(R("NB0"), R("NB0"), 0.0625, OP.mult)
+        for s in range(8):
+            act(R("NB8", 256 * s, 256 * s + 256), R("NB0"), AF.Identity, 16.0 * s, 0.0625)
         ts(R("TN"), R("TN"), -1.0, OP.mult)
         for j in range(3):
             tc(R("ilB", 16 * j, 16 * j + 16), R("il"))
@@ -425,6 +430,9 @@ def rank_program(g, core, T, topo):
         ms(R("ww"), 1.0)
         ts(R("TR"), R("il"), 3584.0, OP.add)
         ts(R("TL2"), R("il"), 320.0, OP.add)
+        ts(R("TRB"), R("il"), 1537.0, OP.add)
+        for s in range(8):
+            ts(R("NF8", 16 * s, 16 * s + 16), R("il"), 1536.0 + 256.0 * s - 2047.0, OP.add)
         for t in range(4):
             ts(R("CT", 16 * t, 16 * t + 16), R("il"), -1.0, OP.mult, 80.0 * t - 320.0, OP.add)
         ms(row("CM128", 0, 128), 128.0)
@@ -439,6 +447,7 @@ def rank_program(g, core, T, topo):
         ts(R("th16"), R("pL", 0, 16), 16.0, OP.mult)
 
     MID = ("pC", T.pC[:, 8:16, :], 256, 512, 1)
+    PB, PQ = R("pQ", 0, 256), R("pQ", 256, 512)
     CT3 = ("cT", T.cT[:], 0, 256, 1)
     AW, CW = R("A"), R("C")
 
@@ -461,9 +470,10 @@ def rank_program(g, core, T, topo):
         lay("pL", 64, "CNM", "Z1")
 
     def set_act(src):
+        if src:
+            tc(R("FL", 0, 16), src)
         for j in range(3):
-            act(R("act3", 16 * j, 16 * j + 16), src, AF.Copy)
-        act(R("FL", 0, 16), src, AF.Copy)
+            mm(R("pE", 112 + 16 * j, 128 + 16 * j), R("ID"), R("FL", 0, 16), True, True)
 
     def keys(ph, c0, c1):
         o = R("pK", 256 + 16 * c0, 256 + 16 * c1) if ph == 2 else R("pK", 16 * c0, 16 * c1) if c0 < 8 else R("pB", 256 + 16 * c0, 256 + 16 * c1)
@@ -480,9 +490,10 @@ def rank_program(g, core, T, topo):
         tt(R("E", 256 * a, 256 * b), ind(AW, R(lst, 16 * a, 16 * b)), R("X16", 256 * a, 256 * b), OP.subtract)
         lab[0] = ""
 
-    def vabs(ph, a, b):
+    def vabs(ph, a, b, k=True):
         act(D3(a, b), R("E", 256 * a, 256 * b), AF.Abs)
-        keys(ph, a, b)
+        if k:
+            keys(ph, a, b)
 
     def sgather(lst, a, b):
         n = 256 * (b - a)
@@ -491,34 +502,23 @@ def rank_program(g, core, T, topo):
 
     def sabs(ph, a, b):
         act(D3(a, b), R("pX", 0, 256 * (b - a)), AF.Abs)
-        keys(ph, a, b)
 
-    def onehot(bank, k1, k2, h):
+    def onehot():
+        o = R("pQ")
+
         def run():
-            mm(R(bank, 128 * h, 128 * h + 128), row("CK", 0, 128), one(128, 1), True, False)
-            for w, src, last in (("BA", k1, False), ("BB", k2, True)):
+            mm(o, row("CK", 0, 128), one(512, 1), True, False)
+            for w, src in (("BA", "KK"), ("BB", "KK2")):
                 for r in range(16):
-                    mm(R(bank, 128 * h + r, 128 * h + 128, 16), R(w, 128 * r, 128 * r + 128), R(src, 8 * h, 8 * h + 8), False, last and r == 15)
-        grp(run, [row("CK", 0, 128), R("BA"), R("BB"), R(k1, 8 * h, 8 * h + 8), R(k2, 8 * h, 8 * h + 8)], [R(bank, 128 * h, 128 * h + 128)])
-
-    def hlay(c0, src, k2, h):
-        o = R("pL", c0 + 8 * h, c0 + 8 * h + 8)
-
-        def run():
-            for r in range(16):
-                mm(o, R("Z1", 15 - r, 143 - r), R(src, 128 * h + r, 128 * h + 128, 16), r == 0, False)
-            mm(o, R("I4K"), R(k2, 8 * h, 8 * h + 8), False, True)
-        grp(run, [R(src, 128 * h, 128 * h + 128), R("Z1"), R("I4K"), R(k2, 8 * h, 8 * h + 8)], [o])
+                    mm(R("pQ", r, 512, 16), R(w, 128 * r, 128 * r + 128), R(src), False, w == "BB" and r == 15)
+        grp(run, [row("CK", 0, 128), one(512, 1), R("BA"), R("BB"), R("KK"), R("KK2")], [o])
 
     def kh(h, o=0):
         return R("pB", 384 + o, 512) if h else R("pK", o, 128)
 
-    def split16(m, off, dd, kk, kk2, h):
-        src = R(m, 128 * h + off, 128 * h + (128 if off == 15 else 127), 16)
-        e = (8 * h, 8 * h + 8)
-        ts(R(dd, *e), src, 201326592.0, OP.add, -201326592.0, OP.add)
-        tt(R(kk, *e), src, R(dd, *e), OP.subtract)
-        act(R(kk2, *e), R(kk, *e), AF.Square)
+    def split16(src, dd, w):
+        ts(R(dd), src, 201326592.0, OP.add, -201326592.0, OP.add)
+        tt(R("KK", 16 * w, 16 * w + 16), src, R(dd), OP.subtract)
 
     def best(h):
         lab[0] = "best"
@@ -526,23 +526,18 @@ def rank_program(g, core, T, topo):
         e = (8 * h, 8 * h + 8)
         scan(R("m1", *w), R("RS", *w), kh(h), BIG, OP.max, OP.min)
         tt(R("nB", *w), kh(h), R("m1", *w), OP.is_equal)
-        tt(R("zz", 128 * h + 1, 128 * h + 128), kh(h, 1), R("m1", 128 * h, 128 * h + 127), OP.max)
+        tt(R("zz", max(1, 128 * h), 128 * h + 128), kh(h, 1 - h), R("m1", max(0, 128 * h - 1), 128 * h + 127), OP.max)
         ts(R("nN", *w), R("nB", *w), -1.0, OP.mult, 1.0, OP.add)
         tt(R("yB", *w), R("nB", *w), ("pC", T.pC[:, 4 * h:4 * h + 4, :], 128 * h, 128 * h + 128, 1), OP.mult)
         scan(R("sB", *w), R("nN", *w), R("yB", *w), 0.0, OP.mult, OP.add)
         ts(R("bU", *e), R("sB", 128 * h + 15, 128 * h + 128, 16), 2047.0, OP.add)
-        ts(R("bF", *e), R("sB", 128 * h + 15, 128 * h + 128, 16), 2047.0, OP.add)
-        split16("m1", 15, "d16", "kk", "kk2", h)
-        onehot("pB", "kk", "kk2", h)
         lab[0] = ""
 
-    def second(h):
+    def second():
         lab[0] = "sec"
-        a, b = 128 * h, 128 * h + 128
-        scan(R("m2", a, b - 1), R("RS2", 1, 128), R("zz", a + 1, b), BIG, OP.max, OP.min)
-        split16("m2", 14, "q16", "kq", "kq2", h)
-        lab[0] = "oq"
-        onehot("pQ", "kq", "kq2", h)
+        scan(R("m2", 0, 255), R("RS2", 1, 256), R("zz", 1, 256), BIG, OP.max, OP.min)
+        split16(R("m1", 15, 256, 16), "d16", 0)
+        split16(R("m2", 14, 255, 16), "q16", 1)
         lab[0] = ""
 
     def bgather(h):
@@ -554,22 +549,29 @@ def rank_program(g, core, T, topo):
         lab[0] = "sg"
         w, e = (128 * h, 128 * h + 128), (8 * h, 8 * h + 8)
         act(R("AB", *w), ind(AW, R("bU", *e)), AF.Copy)
-        act(R("dtf", *w), ind(CW, R("bU", *e)), AF.Identity, -127.9375, 0.0625)
         lab[0] = ""
 
-    def qlist(h):
+    def qlist():
+        lab[0] = "oq"
+        act(R("KK2"), R("KK"), AF.Square)
+        onehot()
         lab[0] = "ql"
-        w, e = (128 * h, 128 * h + 128), (8 * h, 8 * h + 8)
-        tt(R("ZQ", *w), R("pQ", *w), R("ct", *w), OP.min)
-        hlay(16, "ZQ", "kq2", h)
-        ts(R("qU", *e), R("pL", 16 + 8 * h, 24 + 8 * h), 16.0, OP.mult, 1363967.0, OP.add)
+        tt(R("ZQ"), PQ, R("ct"), OP.min)
+        o = R("pL", 16, 32)
+
+        def run():
+            for r in range(16):
+                mm(o, R("Z1", 15 - r, 143 - r), R("ZQ", r, 256, 16), r == 0, False)
+            mm(o, R("I4K"), R("KK2", 16, 32), False, True)
+        grp(run, [R("ZQ"), R("Z1"), R("I4K"), R("KK2", 16, 32)], [o])
+        ts(R("qU"), o, 16.0, OP.mult, 1363967.0, OP.add)
         lab[0] = ""
 
     def transp():
         return g.vector.transpose(T.cT[:], T.cH[:])
 
-    def children(lst):
-        tc(R("cU"), ind(CW, R(lst)))
+    def children(lst, win=None):
+        tc(R("cU"), ind(win or CW, R(lst)))
         ts(R("cH"), R("cU"), -2047.0, OP.add)
         emit("v", transp, CT3, (R("cH"),), 136.0)
 
@@ -593,37 +595,36 @@ def rank_program(g, core, T, topo):
         if s == 0:
             setup2()
         sabs(1, 14, 16)
-        vabs(1, 4, 6)
+        vabs(1, 4, 6, False)
         sgather("cU", 6, 8)
         sabs(1, 6, 8)
+        keys(1, 4, 8)
         vdiff(1, "cU", 8, 12)
         best(0)
         vdiff(1, "cU", 12, 14)
         vabs(1, 8, 12)
-        vabs(1, 12, 14)
+        vabs(1, 12, 14, False)
+        keys(1, 12, 16)
         if s == 0:
             setup3()
-        act(R("NBS"), R("NB0"), AF.Identity, 16.0 * s, 1.0)
         pn = R("pN", 0, 256)
         mms((pn, R("T2"), R("EM")), (pn, one(128, 1), row("LOI")), (pn, R("HIL", 128 * s, 128 * s + 128, 1, 1), one(256, 1)))
         lay("pE", 16, "EM", "Z1")
-        second(0)
         bgather(0)
         best(1)
         vdiff(2, "dU", 0, 4)
         sgather("dU", 6, 8)
         tt(R("CC", 256, 512), pn, R("ct"), OP.min)
-        ts(R("room"), R("pE", 16, 32), 0.0, OP.is_gt)
-        second(1)
+        second()
         bgather(1)
         vdiff(2, "dU", 4, 6)
         vabs(2, 0, 4)
         sabs(2, 6, 8)
         sgath(0)
-        vabs(2, 4, 6)
+        vabs(2, 4, 6, False)
+        keys(2, 4, 8)
         vdiff(2, "dU", 8, 12)
-        qlist(0)
-        qlist(1)
+        qlist()
         if s == 0:
             spread("pN", 0, "BC", "vS")
             pairs_front()
@@ -632,41 +633,50 @@ def rank_program(g, core, T, topo):
             ts(R("act0"), R("pL", 64, 80), 0.0, OP.is_equal)
             set_act(R("act0"))
         vabs(2, 8, 12)
+        sgather("dU", 14, 16)
+        sabs(2, 14, 16)
         sgath(1)
         lab[0] = "em"
         act(R("AQ"), ind(AW, R("qU")), AF.Copy)
         mms((MID, R("ID"), R("AB")), (MID, R("ID"), R("AQ")), (MID, row("CMH", 0, 128), one(256, 1)))
         lab[0] = ""
-        tt(R("c2"), R("ct"), R("pB", 0, 256), OP.max)
-        vdiff(2, "dU", 12, 16)
-        tt(R("pB", 256, 512), R("pB", 0, 256), R("NBS"), OP.min)
-        tt(R("yy"), R("pQ", 0, 256), R("ct"), OP.max)
-        tt(R("CC", 0, 256), R("pB", 256, 512), R("yy"), OP.max)
-        act(R("SBN"), R("pB", 0, 256), AF.Sign, 0.0, -1.0)
-        act(R("SQN"), R("pQ", 0, 256), AF.Sign, 0.0, -1.0)
+        tt(R("c2"), R("ct"), PB, OP.max)
+        vdiff(2, "dU", 12, 14)
+        tt(R("pB", 0, 256), PB, R("NB8", 256 * s, 256 * s + 256), OP.min)
+        tt(R("yy"), PQ, R("ct"), OP.max)
+        tt(R("CC", 0, 256), R("pB", 0, 256), R("yy"), OP.max)
+        lab[0] = "sn"
+        act(R("SGN"), R("pQ"), AF.Sign, 0.0, -1.0)
+        lab[0] = ""
         act(R("pE", 256, 512), R("c2"), AF.Identity, 524160.0, -4096.0)
-        vabs(2, 12, 16)
+        vabs(2, 12, 14, False)
+        keys(2, 12, 16)
         lab[0] = "em"
         ts(R("M2"), MID, 25165824.0, OP.add, -25165824.0, OP.add)
         mms((MID, R("ID"), R("M2")), (MID, R("IN2"), R("X")))
         act(R("AM"), MID, AF.Abs, 0.0, 0.5)
         lay("pL", 32, "AM", "Z16")
         lab[0] = ""
+        lab[0] = "cl"
         px = R("pX", 256, 512)
         mms((px, R("ID"), R("X")), (px, R("IN"), R("AB")))
         ts(R("CLP"), px, -4.0, OP.max, 4.0, OP.min)
+        lab[0] = "cn"
         pg = R("pN", 256, 512)
-        mms((pg, R("IN128"), R("SBN")), (pg, R("IN128"), R("SQN")), (pg, R("IN16"), R("cH")), (pg, row("CM128", 0, 128), one(256, 1)))
+        mms((pg, R("IN128"), R("SGN", 0, 256)), (pg, R("IN128"), R("SGN", 256, 512)), (pg, R("IN16"), R("cH")), (pg, row("CM128", 0, 128), one(256, 1)))
+        lab[0] = "ga"
+        ts(R("dtf"), R("dU"), -2047.0, OP.add, 0.0625, OP.mult)
         tt(R("pE", 256, 512), R("pE", 256, 512), R("dtf"), OP.max)
         tt(R("CC", 512, 768), R("pE", 256, 512), R("c2"), OP.min)
+        lab[0] = "cn"
         act(R("CN", 0, 256), pg, AF.Relu)
+        lab[0] = ""
         tt(R("m3l", 0, 16), R("vF"), R("TR"), OP.subtract)
         ts(R("m3l", 32, 48), R("m3l", 0, 16), -1.0, OP.mult, float(n0 - 3584), OP.add)
-        ts(R("nF"), R("il"), float(n0), OP.add)
-        tt(R("m3l", 16, 32), R("bF"), R("nF"), OP.subtract)
-        tt(R("vact"), R("m3l", 0, 16), R("act3", 0, 16), OP.mult)
+        tt(R("m3l", 16, 32), R("sB", 15, 256, 16), R("NF8", 16 * s, 16 * s + 16), OP.subtract)
+        tt(R("vact"), R("m3l", 0, 16), R("FL", 0, 16), OP.mult)
         tt(R("vact"), R("vact"), R("TR"), OP.add)
-        tt(R("hb"), R("bF"), R("TR"), OP.subtract)
+        tt(R("hb"), R("sB", 15, 256, 16), R("TRB"), OP.subtract)
         tt(R("a2"), R("pL", 32, 48), R("d16"), OP.min)
         scan(R("m3"), R("RS"), R("pK", 256, 512), BIG, OP.max, OP.min)
         es = R("m3", 15, 256, 16)
@@ -676,18 +686,20 @@ def rank_program(g, core, T, topo):
         tt(R("h3", 16, 32), R("a2"), R("a1"), OP.is_le)
         tt(R("h3", 32, 48), R("th16"), R("uu"), OP.is_lt)
         tt(R("h3", 0, 16), R("d16"), R("t1"), OP.is_le)
-        tt(R("FL", 16, 64), R("h3"), R("act3"), OP.mult)
+        tt(R("FL", 16, 64), R("h3"), R("pE", 112, 160), OP.mult)
         actB, hostA, hmA, newA, nrA = [R("FL", 16 * j, 16 * j + 16) for j in range(5)]
         tt(R("p3", 16, 48), R("FL", 16, 48), R("m3l", 16, 48), OP.mult)
         tt(R("vF"), R("vF"), R("p3", 16, 32), OP.add)
         tt(R("vF"), R("vF"), R("p3", 32, 48), OP.add)
         ts(R("vS"), R("vF"), -2048.0, OP.add)
-        tt(nrA, newA, R("room"), OP.mult)
+        tt(nrA, newA, R("pE", 16, 32), OP.min)
         spread("pN", 0, "BC", "vS")
         o = R("pE", 64, 112)
         o0, o1, o2 = R("pE", 64, 80), R("pE", 80, 96), R("pE", 96, 112)
+        lab[0] = "sp"
         mms((o, R("ID"), R("ilB")), (o, R("ID"), R("CST")), (o0, R("I512"), actB), (o0, R("IN512"), hmA), (o0, R("IN256"), newA), (o1, R("IN512"), hmA),
             (o1, R("I512"), hostA), (o1, R("IN256"), nrA), (o2, R("IN256"), hmA), (o2, R("I512"), hostA), (o2, R("IN256"), hostA))
+        lab[0] = ""
         tt(R("nrst"), R("nrst"), newA, OP.subtract)
         ts(R("w0"), hostA, 255.0, OP.mult)
         tt(R("ww"), R("nrst"), R("w0"), OP.add)
@@ -695,13 +707,16 @@ def rank_program(g, core, T, topo):
         tt(R("p3", 0, 16), R("vact"), R("p3", 0, 16), OP.subtract)
         tc(R("vsU"), R("p3", 0, 16))
         pairs_front()
-        lab[0] = "sl"
+        lab[0] = "su"
         tc(R("slU"), o)
+        lab[0] = "sl"
         act(R("selc"), ind(R("CC"), R("slU", 0, 16)), AF.Copy)
-        lab[0] = ""
+        lab[0] = "cb"
         act(R("C", n0, n0 + 256), ind(R("CN"), R("slU", 32, 48)), AF.Identity, 4095.0, -16.0)
+        lab[0] = "ab"
         act(R("CA", 0, 256), R("M2"), AF.Copy, 0.0, 0.5)
         act(R("A", n0, n0 + 256), ind(R("CA"), R("slU", 16, 32)), AF.Copy)
+        lab[0] = ""
         pairs_count()
         tc(R("vU"), R("vF"))
         tt(R("hb"), R("hb"), hostA, OP.mult)
@@ -716,20 +731,23 @@ def rank_program(g, core, T, topo):
         tt(R("ap"), R("ap"), R("TR"), OP.add)
         tc(R("asU"), R("ap"))
         tt(ind(AW, R("asU")), R("AB"), R("CLP"), OP.add)
+        lab[0] = "re" if t == 3 else ""
         tt(R("OV", 16 * t, 16 * t + 16), newA, nrA, OP.subtract)
+        lab[0] = ""
         if t < 3:
             ts(R("w0"), R("pL", 64, 80), 0.0, OP.is_equal)
-            tt(R("w0"), R("w0"), R("nrst"), OP.mult)
-            set_act(R("w0"))
+            tt(R("FL", 0, 16), R("w0"), R("nrst"), OP.mult)
+            set_act(None)
 
     def round_end(p):
         PK, LD = "PK%d" % p, "LD%d" % p
+        lab[0] = "re"
         ts(R("rest"), R("nrst"), -1.0, OP.mult, 1.0, OP.add)
         tc(R("OV", 64, 80), R("rest"))
         scan(R("SC"), R("SCM"), R("OV"), 0.0, OP.mult, OP.add)
-        mms((R("pX", 0, 80), R("BLK"), R("SC")), (R("pX", 0, 80), R("TN"), R("OV")))
-        mm(R("pX", 80, 84), R("BLK"), R("SC", 15, 64, 16), True, True)
-        tc(R("P5"), R("pX", 0, 80))
+        mms((R("pB", 256, 336), R("BLK"), R("SC")), (R("pB", 256, 336), R("TN"), R("OV")))
+        mm(R("pB", 336, 340), R("BLK"), R("SC", 15, 64, 16), True, True)
+        tc(R("P5"), R("pB", 256, 336))
         ts(R("q1", 0, 64), R("P5", 0, 64), 64.0, OP.is_lt)
         tt(R("q1", 0, 64), R("q1", 0, 64), R("OV", 0, 64), OP.mult)
         tt(R("q3", 0, 64), R("P5", 0, 64), R("CT", 0, 64), OP.add)
@@ -739,7 +757,7 @@ def rank_program(g, core, T, topo):
         tt(R("l1"), R("l1"), R("TL2"), OP.add)
         tc(R("ovU"), R("l1"))
         tc(ind(R(PK), R("ovU")), R("X"))
-        ts(R(PK, 64, 320, 80), R("pX", 80, 84), 64.0, OP.min)
+        ts(R(PK, 64, 320, 80), R("pB", 336, 340), 64.0, OP.min)
         tr = []
         for t in range(4):
             dst = T.cores[(rank + 1 + (4 * p + t) % (nrank - 1)) % nrank]
@@ -754,6 +772,7 @@ def rank_program(g, core, T, topo):
             clocks[("ra%d" % p, 8)] = {}
             acc.setdefault(LD, []).append((True, 0, 320, 1, "ra%d" % p, 8, "remote"))
         rec("g", send, [R(LD, 0, 320)], [R(PK, 0, 320)], 1500.0, 2500.0)
+        lab[0] = ""
         act(R("AV"), ind(AW, R("vU")), AF.Copy)
         pn = R("pN", 0, 256)
         mms((pn, R("ID"), R("X")), (pn, R("IN"), R("AV")))
@@ -778,7 +797,7 @@ def rank_program(g, core, T, topo):
     tc(R("vU"), R("topU"))
     tc(R("vF"), R("topF", 0, 16))
     ts(R("vS"), R("vF"), -2048.0, OP.add)
-    children("topU")
+    children("topU", R("KI"))
     for p in range(2):
         if p:
             newx()
@@ -789,8 +808,8 @@ def rank_program(g, core, T, topo):
         for t in range(4):
             step(4 * p + t)
         if p:
-            dma("y", T.yc[:], T.C[:, 0:3584], [], [R("C", 0, 3584)])
-            dma("y", T.ya[:], T.A[:, 0:3584], [], [R("A", 0, 3584)])
+            dma("y", T.yc[:], T.C[:, 0:3584], [], [R("C", 0, 3584)], 14000.0)
+            dma("y", T.ya[:], T.A[:, 0:3584], [], [R("A", 0, 3584)], 7000.0)
         round_end(p)
     dma("y", T.yx[:], T.X[:], [], [R("X")])
     flush()

from concourse.bass import DstId, RemoteDMATransfer
from concourse.mybir import dt, AluOpType, ActivationFunctionType
OP = AluOpType
AF = ActivationFunctionType
B2, F4, H2, I4, U2 = "bfloat16", "float32", "float16", "int32", "uint16"
BIG = 1.0e9
PEC, WAKE = 0.52, 75.0
PRI = {"re": 30000, "sl": 20000, "em": 3000, "ql": 6000, "bg": 3000, "sg": -1500, "v21": -1500, "v20": -1500, "v11": -3000, "oq": 20000, "v10": -3000, "sec": -1500,
       "sp": 20000, "cn": -3000}
TOT = [0.0]
SCRATCH = {}


PART = {}


def sb(dtype, n, *names):
    if len(names) > 2 and n <= 256:
        big = "w%d%s" % (n, dtype)
        SCRATCH[big] = ("sbuf", [128, n * len(names)], dtype)
        for j, k in enumerate(names):
            PART[k] = (big, n * j, n)
    else:
        for k in names:
            SCRATCH[k] = ("sbuf", [128, n], dtype)


def info(name):
    return SCRATCH[PART[name][0] if name in PART else name]


sb(B2, 4096, "A", "X16", "E", "IND")
sb(F4, 4096, "C")
sb(B2, 512, "G")
sb(B2, 2048, "ONE", "BC", "BA", "BB", "TB")
sb(B2, 128, "BLK", "ID", "IN", "IN2", "I4K", "IN128", "IN16", "I512", "IN512", "IN256", "TN", "T2", "TA", "CK", "CM128", "CMH", "KW", "S00", "S01", "S10", "S11")
sb(B2, 144, "Z1", "Z16")
sb(B2, 256, "X")
sb(B2, 256, "KC", "LOI", "EM", "M2", "AM", "AB", "CLP", "CNM", "AV", "AQ", "nB", "nN")
sb(F4, 256, "NB0", "RS", "RS2", "ct", "dtf", "m1", "m2", "m3", "zz", "c2", "yy", "selc", "tmpf", "yB", "sB")
sb(H2, 256, "ZQ", "cH")
sb(U2, 256, "cU", "dU", "vBU")
sb(I4, 1536, "KI")
sb(F4, 768, "CC")
sb(F4, 2048, "NB8")
sb(F4, 128, "NF8")
sb(B2, 512, "SGN")
sb(F4, 512, "CN")
sb(B2, 768, "CA")
sb(F4, 16, "il", "TRB", "vact", "TR", "TL2", "vF", "d16", "q16", "th16", "rest", "nrst", "a1", "a2", "t1", "uu", "act0", "w0", "ww", "hb", "ap",
   "l1", "l2", "l3", "l4", "cnt4", "cum4", "gap4", "PF", "RI", "RM", "LM", "HU")
sb(B2, 32, "KK", "KK2")
sb(H2, 16, "vS")
sb(U2, 16, "vU", "topU", "bU", "qU", "vsU", "asU", "ovU", "dlU")
sb(I4, 16, "IT", "IT2", "IT3")
sb(I4, 16, "TPI")
sb(B2, 48, "ilB", "CST")
sb(F4, 48, "h3", "m3l", "p3", "topF")
sb(U2, 48, "slU")
sb(B2, 80, "FL", "SCM", "OV", "SC")
sb(F4, 80, "CT", "P5", "q1", "q3")
sb(B2, 576, "PK0", "PK1", "LD0", "LD1")
SCRATCH["D"] = ("sbuf", [128, 16, 256], B2)
SCRATCH["cT"] = ("sbuf", [128, 8, 32], H2)
SCRATCH["HIL"] = ("sbuf", [1, 1024], B2)
SCRATCH["THI"] = ("sbuf", [8, 256], I4)
SCRATCH["TH8"] = ("sbuf", [8, 256], F4)
SCRATCH["ZU"] = ("sbuf", [8, 144], F4)
PSUM = ("pK", "pB", "pQ", "pL", "pE", "pN", "pX", "pC")
for _b in PSUM[:7]:
    SCRATCH[_b] = ("psum", [128, 512], F4)
SCRATCH["pC"] = ("psum", [128, 16, 32], F4)
SEMAPHORES = ["sv", "st", "ss", "sg", "ra0", "ra1", "rl"] + ["dm%d" % i for i in range(16)]


def rank_program(g, core, T, topo):
    rank = T.rank_of(core)
    if rank is None:
        return
    nrank = len(T.cores)
    Q = {"v": g.vector, "t": g.tensor, "s": g.scalar, "g": g, "y": g.sync}
    SEM = {"v": "sv", "t": "st", "s": "ss", "g": "sg"}
    count = {k: 0 for k in SEM.values()}
    know = {q: {} for q in Q}
    clocks = {}
    acc = {}
    ndma = [0]
    prog = []
    lab = [""]
    group = []

    def R(name, c0=0, c1=None, st=1, p=128):
        buf, o, n = PART[name] if name in PART else (name, 0, SCRATCH[name][1][1])
        if c1 is None:
            c1 = n
        t = T[buf]
        return (name, t[0:p, o + c0:o + c1:st] if st > 1 else t[0:p, o + c0:o + c1], c0, c1, st)

    def D3(c0, c1, k0=0, k1=256):
        return ("D", T.D[:, c0:c1, k0:k1], 256 * c0, 256 * c1, 1)

    def apart(a, b):
        if a[1] >= b[2] or b[1] >= a[2]:
            return True
        return a[3] == b[3] and a[3] > 1 and (a[1] - b[1]) % a[3] != 0

    def order(q, reads, writes):
        need = {}
        for is_w, lst in ((False, reads), (True, writes)):
            for (name, _, c0, c1, st) in lst:
                me = (is_w, c0, c1, st)
                for rec_ in acc.get(name, ()):
                    if name in PSUM:
                        if rec_[6] == q and (q == "t" or not (is_w or rec_[0]) or apart(me, rec_)):
                            continue
                    elif not (is_w or rec_[0]) or apart(me, rec_):
                        continue
                    if know[q].get(rec_[4], 0) < rec_[5]:
                        need[rec_[4]] = max(need.get(rec_[4], 0), rec_[5])
        for s in list(need):
            for o in list(need):
                if o != s and need[s] and clocks[(s, need[s])].get(o, 0) >= need.get(o, 0):
                    need[o] = 0
        for s, n in need.items():
            if n:
                Q[q].wait_ge(T.sem[s], n)
                for k, x in clocks[(s, n)].items():
                    know[q][k] = max(know[q].get(k, 0), x)
                know[q][s] = max(know[q].get(s, 0), n)

    def note(q, sem, n, reads, writes):
        clocks[(sem, n)] = dict(know[q])
        for is_w, lst in ((False, reads), (True, writes)):
            for (name, _, c0, c1, st) in lst:
                old = acc.get(name, [])
                if is_w:
                    old = [r for r in old if not (c0 <= r[1] and r[2] <= c1 and st == 1 and (name not in PSUM or r[6] == q))]
                else:
                    old = [r for r in old if not (not r[0] and r[6] == q and c0 <= r[1] and r[2] <= c1 and st == 1)]
                old.append((is_w, c0, c1, st, sem, n, q))
                acc[name] = old

    def rec(q, run, writes, reads, cost, lat=0.0):
        prog.append((q, run, reads, writes, cost, lat, PRI.get(lab[0], 0.0)))

    def nel(o):
        if o[0] == "ind":
            return 16 * (o[2][3] - o[2][2])
        return (o[3] - o[2] + o[4] - 1) // o[4]

    def small(o):
        return o[0] != "ind" and info(o[0])[0] == "sbuf" and info(o[0])[2] in (B2, H2, U2)

    def vcost(out, ins, full):
        if out[0] == "ind":
            return 60.0 + 4.0 * nel(out)
        for o in ins:
            if o[0] == "ind":
                return 60.0 + 1.6 * nel(o)
        if full:
            return max(66.0, (2.07 if all(info(o[0])[0] == "sbuf" for o in ins) else 1.04) * nel(out))
        return max(66.0, (0.52 if all(small(o) for o in list(ins) + [out]) else 1.04) * nel(out))

    def flush():
        n = len(prog)
        preds = [{} for _ in range(n)]
        hist = {}
        for i, (q, run, reads, writes, cost, lat, pri) in enumerate(prog):
            for is_w, lst in ((False, reads), (True, writes)):
                for (name, _, c0, c1, st) in lst:
                    me = (is_w, c0, c1, st)
                    for r in hist.get(name, ()):
                        far = apart(me, r)
                        if name in PSUM:
                            hit = (q != r[4]) or (not far and (is_w or r[0]))
                        else:
                            hit = not far and (is_w or r[0])
                        if hit and r[5] != i:
                            preds[i][r[5]] = True
            for is_w, lst in ((False, reads), (True, writes)):
                for (name, _, c0, c1, st) in lst:
                    old = hist.get(name, [])
                    if is_w:
                        old = [r for r in old if not (c0 <= r[1] and r[2] <= c1 and st == 1 and (name not in PSUM or r[4] == q))]
                    old.append((is_w, c0, c1, st, q, i))
                    hist[name] = old
        succ = [[] for _ in range(n)]
        for i in range(n):
            for p in preds[i]:
                succ[p].append(i)
        tail = [0.0] * n
        for i in range(n - 1, -1, -1):
            tail[i] = prog[i][4] + prog[i][5] + max([tail[j] + (WAKE if prog[j][0] != prog[i][0] else 15.0) for j in succ[i]] + [0.0])
        left = [len(p) for p in preds]
        ready = {q: [] for q in Q}
        for i in range(n):
            if not left[i]:
                ready[prog[i][0]].append((0.0, i))
        free = {q: 0.0 for q in Q}
        at = {}
        seq = []
        while len(seq) < n:
            pick = None
            for q in Q:
                if ready[q]:
                    t = max(free[q], min(r[0] for r in ready[q]))
                    if pick is None or t < pick[0]:
                        pick = (t, q)
            t, q = pick
            r = max([r for r in ready[q] if r[0] <= t + 1e-6], key=lambda z: tail[z[1]] + prog[z[1]][6])
            ready[q].remove(r)
            i = r[1]
            free[q] = t + prog[i][4]
            seq.append(i)
            fin = t + prog[i][4] + prog[i][5]
            for j in succ[i]:
                at[j] = max(at.get(j, 0.0), fin + (WAKE if prog[j][0] != q else 15.0))
                left[j] -= 1
                if not left[j]:
                    ready[prog[j][0]].append((at[j], j))
        TOT[0] = max(free.values())
        for i in seq:
            q, run, reads, writes, cost, lat, pri = prog[i]
            run(q, reads, writes)

    def single(make):
        def run(q, reads, writes):
            order(q, reads, writes)
            s = SEM[q]
            for m in make:
                count[s] += 1
                m().then_inc(T.sem[s], 1)
            note(q, s, count[s], reads, writes)
        return run

    def dma(q, out, in_, writes, reads, lat=2500.0):
        s = "dm%d" % ndma[0]
        ndma[0] += 1

        def run(q_, rds, wrs):
            order(q_, rds, wrs)
            Q[q_].dma_start(out, in_).then_inc(T.sem[s], 16)
            note(q_, s, 16, rds, wrs)
        rec(q, run, writes, reads, 60.0, lat)

    def ind(win, off):
        return ("ind", win, off)

    def ap(o):
        return o[1][1].indirect(o[2][1]) if o[0] == "ind" else o[1]

    def rd(*os):
        out = []
        for o in os:
            if isinstance(o, tuple):
                out += [o[1], o[2]] if o[0] == "ind" else [o]
        return out

    def sc(x):
        return x[1] if isinstance(x, tuple) else x

    def emit(q, make, out, ins, cost):
        i = out[0] == "ind"
        rec(q, single([make]), [out[1]] if i else [out], rd(*ins) + ([out[2]] if i else []), cost)

    def tt(out, a, b, op):
        emit("v", lambda: g.vector.tensor_tensor(ap(out), ap(a), ap(b), op), out, (a, b), vcost(out, (a, b), True))

    def ts(out, a, s1, op0, s2=None, op1=None):
        c = vcost(out, (a,), False)
        if op1 is None:
            emit("v", lambda: g.vector.tensor_scalar(ap(out), ap(a), sc(s1), None, op0), out, (a, s1), c)
        else:
            emit("v", lambda: g.vector.tensor_scalar(ap(out), ap(a), sc(s1), sc(s2), op0, op1), out, (a, s1, s2), c)

    def tc(out, a):
        emit("v", lambda: g.vector.tensor_copy(ap(out), ap(a)), out, (a,), vcost(out, (a,), False))

    def ms(out, x):
        emit("v", lambda: g.vector.memset(ap(out), x), out, (), vcost(out, (), False))

    def scan(out, d0, d1, init, op0, op1):
        emit("v", lambda: g.vector.tensor_tensor_scan(ap(out), ap(d0), ap(d1), init, op0, op1), out, (d0, d1), vcost(out, (d0, d1), False))

    def act(out, a, f, bias=0.0, scale=1.0):
        emit("s", lambda: g.scalar.activation(ap(out), ap(a), f, bias=bias, scale=sc(scale)), out, (a, scale),
             80.0 + max(64.0, (1.5 if a[0] == "ind" else 1.0) * nel(out)) * 1.04)

    def mm(out, l, r, start, stop):
        c = ((lambda: g.tensor.matmul(out[1], l[1], r[1], start, stop)), [l, r], out, max(64, nel(out)) * PEC * (4 if info(l[0])[2] == F4 else 1))
        if group:
            group[-1].append(c)
        else:
            rec("t", single([c[0]]), [out], [l, r], c[3])

    def grp(fn, rds=None, wrs=None):
        group.append([])
        fn()
        calls = group.pop()
        reads, writes = [], []
        for c in calls:
            reads += [o for o in c[1] if o not in reads]
            if c[2] not in writes:
                writes.append(c[2])
        rec("t", single([c[0] for c in calls]), wrs or writes, rds or reads, sum(c[3] for c in calls))

    def mms(*calls):
        def run():
            for n, (o, l, r) in enumerate(calls):
                mm(o, l, r, n == 0, n == len(calls) - 1)
        grp(run)

    def sel(out, in_, pat, op, base, cm, fill=0.0):
        emit("g", lambda: g.affine_select(ap(out), ap(in_), pat, op, fill, base, cm), out, (in_,), 170.0 + 2.1 * nel(out))

    def iota(out, pat, base, cm):
        emit("g", lambda: g.iota(ap(out), pat, base, cm, allow_small_or_imprecise_dtypes=True), out, (), 130.0 + 2.1 * nel(out))

    def lay(out, c0, src, z):
        def run():
            for r in range(16):
                mm(R(out, c0, c0 + 16), R(z, 15 - r, 143 - r), R(src, r, 256, 16), r == 0, r == 15)
        grp(run, [R(src, 0, 256), R(z)], [R(out, c0, c0 + 16)])

    def spread(out, c0, w, src):
        def run():
            for r in range(16):
                mm(R(out, c0 + r, c0 + 256, 16), R(w, 128 * r, 128 * r + 128), R(src, 0, 16), True, True)
        grp(run, [R(w), R(src, 0, 16)], [R(out, c0, c0 + 256)])

    def one(n, p=128):
        return R("ONE", 0, n, 1, p)

    def row(nm, a=0, b=256):
        return R(nm, a, b, 1, 1)

    dma("y", T.TPI[:], T.tops[:], [R("TPI")], [])
    dma("s", T.X[:], T.x0[:], [R("X")], [])
    dma("y", T.KI[:, 0:768], T.kids[:, 0:768], [R("KI", 0, 768)], [])
    dma("s", T.A[:, 0:1536], T.a0[:], [R("A", 0, 1536)], [])
    dma("y", T.KI[:, 768:1536], T.kids[:, 768:1536], [R("KI", 768, 1536)], [])
    dma("y", T.THI[:], T.th[:], [R("THI", p=8)], [])
    ms(R("ONE"), 1.0)
    iota(R("IT"), [[0, 16]], 0, 1)
    iota(R("IT2"), [[16, 16]], 0, 0)
    iota(R("IT3"), [[0, 16]], 0, 1)
    sel(R("BLK"), one(128), [[-16, 8], [0, 16]], OP.is_ge, 0, 1)
    sel(R("BLK"), R("BLK"), [[16, 8], [0, 16]], OP.is_ge, 15, -1)
    iota(R("RI"), [[1, 16]], 0, 0)
    sel(R("Z1"), one(144), [[-16, 9], [0, 16]], OP.is_ge, 0, 1)
    sel(R("Z1"), R("Z1"), [[16, 9], [0, 16]], OP.is_ge, 15, -1)
    sel(R("Z1"), R("Z1"), [[0, 9], [1, 16]], OP.is_equal, -15, 0)
    sel(R("ID"), one(128), [[-1, 128]], OP.is_equal, 0, 1)
    iota(row("LOI"), [[0, 16], [2, 16]], -15, 0)
    iota(R("KW"), [[0, 8], [512, 16]], -3840, 0)
    sel(R("TA"), R("BLK"), [[1, 128]], OP.is_ge, -1, -1)
    iota(row("tmpf"), [[1, 256]], 1, 0)
    ms(R("RS"), -BIG)
    sel(R("RS2"), R("RS"), [[0, 16], [1, 16]], OP.not_equal, -1, 0, BIG)
    sel(R("RS"), R("RS"), [[0, 16], [1, 16]], OP.not_equal, 0, 0, BIG)
    iota(R("NB0"), [[1, 256]], -511, 0)
    ms(R("ZU", p=8), 1.0)
    sel(R("ZU", p=8), R("ZU", p=8), [[1, 144]], OP.is_equal, -15, -16)
    sel(R("SCM"), one(80), [[0, 5], [1, 16]], OP.not_equal, 0, 0)
    sel(R("TN"), R("BLK"), [[-1, 128]], OP.is_ge, 0, 1)
    ms(R("A", 1536, 3840), 0.0)
    ms(R("A", 3840, 4096), 8192.0)
    ts(R("IT"), R("IT"), 15, OP.bitwise_and)
    tt(R("il"), R("IT"), R("IT2"), OP.add)
    tc(R("PF"), R("IT"))
    ts(R("IT3"), R("IT3"), 16, OP.bitwise_and)
    tc(R("HU", 1, 2), R("IT3", 0, 1))
    ts(R("HU", 1, 2), R("HU", 1, 2), 0.0625, OP.mult)
    ts(R("HU", 0, 1), R("HU", 1, 2), -1.0, OP.mult, 1.0, OP.add)
    tc(R("topU"), R("TPI"))
    tc(R("topF", 0, 16), R("TPI"))

    def newx():
        for k in range(16):
            o = R("X16", k, 4096, 16)
            if k % 3 == 2:
                act(o, R("X"), AF.Copy)
            else:
                tc(o, R("X"))
        act(R("CA", 256, 512), R("X"), AF.Copy)

    newx()
    ts(R("RM"), R("RI"), R("PF", 0, 1), OP.is_equal)
    for u in range(2):
        for w in range(2):
            nm = "S%d%d" % (u, w)
            sel(R(nm), R("ID") if u == w else one(128), [[-1, 128]], OP.is_equal, 16 * (w - u), 1)
            ts(R(nm), R(nm), R("HU", u, u + 1), OP.mult)
    ts(R("LM"), R("RI"), R("PF", 0, 1), OP.is_gt)
    act(R("C", 1536, 3584), R("ONE"), AF.Identity, 4095.0, 0.0)
    act(R("C", 3584, 4096), one(512), AF.Identity, 4095.0, 0.0)
    ts(R("Z16"), R("Z1"), 16.0, OP.mult)
    tt(R("KW"), R("KW"), R("BLK"), OP.mult)
    ts(row("KC"), row("LOI"), 0.5, OP.mult)
    tt(row("CK", 0, 128), row("LOI", 0, 128), row("LOI", 0, 128), OP.mult)
    ts(row("CK", 0, 128), row("CK", 0, 128), -64.0, OP.mult, 128.0, OP.add)
    for nm, x in (("IN", -1.0), ("IN256", -256.0)):
        ts(R(nm), R("ID"), x, OP.mult)
    ts(R("TA"), R("TA"), 512.0, OP.mult)
    tt(R("T2"), R("TA"), R("IN256"), OP.add)
    ts(row("LOI"), row("tmpf"), 0.0625, OP.mult)
    ms(R("HIL", 0, 128, 1, 1), 224.0)
    ms(row("CMH", 0, 128), -0.5)
    tc(R("C", 0, 768), R("KI", 0, 768))
    tc(R("C", 768, 1536), R("KI", 768, 1536))

    def setup2():
        for r in range(16):
            act(R("BA", 128 * r, 128 * r + 128), R("KW"), AF.Copy, 0.0, R("RM", r, r + 1))
        for r in range(16):
            ts(R("BC", 128 * r, 128 * r + 128), R("BLK"), R("RM", r, r + 1), OP.mult)
        ts(R("BB"), R("BC"), -256.0, OP.mult)
        for nm, x in (("IN2", -2.0), ("I4K", 4096.0), ("IN128", -128.0), ("IN16", -0.0625), ("I512", 512.0), ("IN512", -512.0)):
            ts(R(nm), R("ID"), x, OP.mult)

    def setup3():
        for r in range(16):
            ts(R("TB", 128 * r, 128 * r + 128), R("BLK"), R("LM", r, r + 1), OP.mult)
        for s in range(8):
            act(R("NB8", 256 * s, 256 * s + 256), R("NB0"), AF.Identity, 16.0 * s, 0.0625)
        ts(R("TN"), R("TN"), -1.0, OP.mult)
        for j in range(3):
            tc(R("ilB", 16 * j, 16 * j + 16), R("il"))
            ms(R("CST", 16 * j, 16 * j + 16), (0.0, 512.0, 256.0)[j])
        ms(R("ww"), 1.0)
        ts(R("TR"), R("il"), 3584.0, OP.add)
        ts(R("TL2"), R("il"), 320.0, OP.add)
        ts(R("TRB"), R("il"), 1537.0, OP.add)
        for s in range(8):
            ts(R("NF8", 16 * s, 16 * s + 16), R("il"), 1536.0 + 256.0 * s - 2047.0, OP.add)
        for t in range(4):
            ts(R("CT", 16 * t, 16 * t + 16), R("il"), -1.0, OP.mult, 80.0 * t - 320.0, OP.add)
        ms(row("CM128", 0, 128), 128.0)
        for s in range(1, 8):
            ms(R("HIL", 128 * s, 128 * s + 128, 1, 1), 224.0 + 16.0 * s)
        ms(R("CA", 512, 768), 0.0)
        ms(R("CN", 256, 512), 0.0)
        ms(R("PK0"), 0.0)
        ms(R("PK1"), 0.0)
        tc(R("TH8", p=8), R("THI", p=8))
        mms(*[(R("pL", 0, 16), R("ZU", 15 - r, 143 - r, 1, 8), R("TH8", r, 256, 16, 8)) for r in range(16)])
        ts(R("th16"), R("pL", 0, 16), 16.0, OP.mult)

    MID = ("pC", T.pC[:, 8:16, :], 256, 512, 1)
    PB, PQ = R("pQ", 0, 256), R("pQ", 256, 512)
    CT3 = ("cT", T.cT[:], 0, 256, 1)
    AW, CW = R("A"), R("C")

    def pairs_front():
        ts(R("vBU"), R("pN", 0, 256), 2048.0, OP.add)
        for c in range(16):
            ts(R("IND", 272 * c, 256 * c + 256), R("vBU", 16 * c, 256), R("vF", c, c + 1), OP.is_equal, R("ww", c, c + 1), OP.mult)

    def pairs_count():
        def run():
            mm(R("pX", 256, 512), R("TB", 0, 128), R("IND", 0, 256), True, False)
            for c in range(15):
                mm(R("pX", 256 + 16 * (c + 1), 512), R("BLK"), R("IND", 272 * c + 16, 256 * c + 256), False, False)
            for r in range(1, 16):
                mm(R("pX", 256 + r, 512, 16), R("TB", 128 * r, 128 * r + 128), R("IND", r, 4096, 272), False, r == 15)
        grp(run, [R("IND"), R("TB"), R("BLK")], [R("pX", 256, 512)])

    def pairs_list():
        act(R("CNM"), R("pX", 256, 512), AF.Copy)
        lay("pL", 64, "CNM", "Z1")

    def set_act(src):
        if src:
            tc(R("FL", 0, 16), src)
        for j in range(3):
            mm(R("pE", 112 + 16 * j, 128 + 16 * j), R("ID"), R("FL", 0, 16), True, True)

    def keys(ph, c0, c1):
        o = R("pK", 256 + 16 * c0, 256 + 16 * c1) if ph == 2 else R("pK", 16 * c0, 16 * c1) if c0 < 8 else R("pB", 256 + 16 * c0, 256 + 16 * c1)

        def run():
            if ph == 1:
                mm(o, R("ONE", 0, 128, 1, 1), row("KC", 16 * c0, 16 * c1), True, False)
            for r in range(16):
                mm(o, R("Z16", 15 - r, 143 - r), D3(c0, c1, 16 * r, 16 * r + 16), ph == 2 and r == 0, r == 15)
        grp(run, [D3(c0, c1), R("Z16")] + ([R("ONE"), row("KC")] if ph == 1 else []), [o])

    def vdiff(ph, lst, a, b):
        lab[0] = "v%d%d" % (ph, a // 8)
        tt(R("E", 256 * a, 256 * b), ind(AW, R(lst, 16 * a, 16 * b)), R("X16", 256 * a, 256 * b), OP.subtract)
        lab[0] = ""

    def vabs(ph, a, b, k=True):
        act(D3(a, b), R("E", 256 * a, 256 * b), AF.Abs)
        if k:
            keys(ph, a, b)

    def sgather(lst, a, b):
        n = 256 * (b - a)
        act(R("G", 0, n), ind(AW, R(lst, 16 * a, 16 * b)), AF.Copy)
        mms((R("pX", 0, n), R("ID"), R("G", 0, n)), (R("pX", 0, n), R("IN"), R("X16", 256 * a, 256 * b)))

    def sabs(ph, a, b):
        act(D3(a, b), R("pX", 0, 256 * (b - a)), AF.Abs)

    def onehot():
        o = R("pQ")

        def run():
            mm(o, row("CK", 0, 128), one(512, 1), True, False)
            for w, src in (("BA", "KK"), ("BB", "KK2")):
                for r in range(16):
                    mm(R("pQ", r, 512, 16), R(w, 128 * r, 128 * r + 128), R(src), False, w == "BB" and r == 15)
        grp(run, [row("CK", 0, 128), one(512, 1), R("BA"), R("BB"), R("KK"), R("KK2")], [o])

    def kh(h, o=0):
        return R("pB", 384 + o, 512) if h else R("pK", o, 128)

    def split16(src, dd, w):
        ts(R(dd), src, 201326592.0, OP.add, -201326592.0, OP.add)
        tt(R("KK", 16 * w, 16 * w + 16), src, R(dd), OP.subtract)

    def best(h):
        lab[0] = "best"
        w = (128 * h, 128 * h + 128)
        e = (8 * h, 8 * h + 8)
        scan(R("m1", *w), R("RS", *w), kh(h), BIG, OP.max, OP.min)
        tt(R("nB", *w), kh(h), R("m1", *w), OP.is_equal)
        tt(R("zz", max(1, 128 * h), 128 * h + 128), kh(h, 1 - h), R("m1", max(0, 128 * h - 1), 128 * h + 127), OP.max)
        ts(R("nN", *w), R("nB", *w), -1.0, OP.mult, 1.0, OP.add)
        tt(R("yB", *w), R("nB", *w), ("pC", T.pC[:, 4 * h:4 * h + 4, :], 128 * h, 128 * h + 128, 1), OP.mult)
        scan(R("sB", *w), R("nN", *w), R("yB", *w), 0.0, OP.mult, OP.add)
        ts(R("bU", *e), R("sB", 128 * h + 15, 128 * h + 128, 16), 2047.0, OP.add)
        lab[0] = ""

    def second():
        lab[0] = "sec"
        scan(R("m2", 0, 255), R("RS2", 1, 256), R("zz", 1, 256), BIG, OP.max, OP.min)
        split16(R("m1", 15, 256, 16), "d16", 0)
        split16(R("m2", 14, 255, 16), "q16", 1)
        lab[0] = ""

    def bgather(h):
        lab[0] = "bg"
        tc(R("dU", 128 * h, 128 * h + 128), ind(CW, R("bU", 8 * h, 8 * h + 8)))
        lab[0] = ""

    def sgath(h):
        lab[0] = "sg"
        w, e = (128 * h, 128 * h + 128), (8 * h, 8 * h + 8)
        act(R("AB", *w), ind(AW, R("bU", *e)), AF.Copy)
        lab[0] = ""

    def qlist():
        lab[0] = "oq"
        act(R("KK2"), R("KK"), AF.Square)
        onehot()
        lab[0] = "ql"
        tt(R("ZQ"), PQ, R("ct"), OP.min)
        o = R("pL", 16, 32)

        def run():
            for r in range(16):
                mm(o, R("Z1", 15 - r, 143 - r), R("ZQ", r, 256, 16), r == 0, False)
            mm(o, R("I4K"), R("KK2", 16, 32), False, True)
        grp(run, [R("ZQ"), R("Z1"), R("I4K"), R("KK2", 16, 32)], [o])
        ts(R("qU"), o, 16.0, OP.mult, 1363967.0, OP.add)
        lab[0] = ""

    def transp():
        return g.vector.transpose(T.cT[:], T.cH[:])

    def children(lst, win=None):
        tc(R("cU"), ind(win or CW, R(lst)))
        ts(R("cH"), R("cU"), -2047.0, OP.add)
        emit("v", transp, CT3, (R("cH"),), 136.0)

        def run():
            for u in range(2):
                for w in range(2):
                    mm(("pC", T.pC[:, 0:8, 16 * u:16 * u + 16], 0, 128, 1), R("S%d%d" % (u, w)), ("cT", T.cT[:, :, 16 * w:16 * w + 16], 0, 256, 1), w == 0, w == 1)
        grp(run, [CT3, R("S00"), R("S01"), R("S10"), R("S11")], [("pC", T.pC[:, 0:8, :], 0, 256, 1)])
        lab[0] = "ch2"
        act(R("ct"), ind(CW, R(lst)), AF.Identity, -127.9375, 0.0625)
        act(R("EM"), R("ct"), AF.Relu, -2047.0, 16.0)
        lab[0] = ""

    def step(s):
        t = s % 4
        n0 = 1536 + 256 * s
        vdiff(1, "cU", 0, 4)
        sgather("cU", 14, 16)
        vdiff(1, "cU", 4, 6)
        vabs(1, 0, 4)
        if s == 0:
            setup2()
        sabs(1, 14, 16)
        vabs(1, 4, 6, False)
        sgather("cU", 6, 8)
        sabs(1, 6, 8)
        keys(1, 4, 8)
        vdiff(1, "cU", 8, 12)
        best(0)
        vdiff(1, "cU", 12, 14)
        vabs(1, 8, 12)
        vabs(1, 12, 14, False)
        keys(1, 12, 16)
        if s == 0:
            setup3()
        pn = R("pN", 0, 256)
        mms((pn, R("T2"), R("EM")), (pn, one(128, 1), row("LOI")), (pn, R("HIL", 128 * s, 128 * s + 128, 1, 1), one(256, 1)))
        lay("pE", 16, "EM", "Z1")
        bgather(0)
        best(1)
        vdiff(2, "dU", 0, 4)
        sgather("dU", 6, 8)
        tt(R("CC", 256, 512), pn, R("ct"), OP.min)
        second()
        bgather(1)
        vdiff(2, "dU", 4, 6)
        vabs(2, 0, 4)
        sabs(2, 6, 8)
        sgath(0)
        vabs(2, 4, 6, False)
        keys(2, 4, 8)
        vdiff(2, "dU", 8, 12)
        qlist()
        if s == 0:
            spread("pN", 0, "BC", "vS")
            pairs_front()
            pairs_count()
            pairs_list()
            ts(R("act0"), R("pL", 64, 80), 0.0, OP.is_equal)
            set_act(R("act0"))
        vabs(2, 8, 12)
        sgather("dU", 14, 16)
        sabs(2, 14, 16)
        sgath(1)
        lab[0] = "em"
        act(R("AQ"), ind(AW, R("qU")), AF.Copy)
        mms((MID, R("ID"), R("AB")), (MID, R("ID"), R("AQ")), (MID, row("CMH", 0, 128), one(256, 1)))
        lab[0] = ""
        tt(R("c2"), R("ct"), PB, OP.max)
        vdiff(2, "dU", 12, 14)
        tt(R("pB", 0, 256), PB, R("NB8", 256 * s, 256 * s + 256), OP.min)
        tt(R("yy"), PQ, R("ct"), OP.max)
        tt(R("CC", 0, 256), R("pB", 0, 256), R("yy"), OP.max)
        lab[0] = "sn"
        act(R("SGN"), R("pQ"), AF.Sign, 0.0, -1.0)
        lab[0] = ""
        act(R("pE", 256, 512), R("c2"), AF.Identity, 524160.0, -4096.0)
        vabs(2, 12, 14, False)
        keys(2, 12, 16)
        lab[0] = "em"
        ts(R("M2"), MID, 25165824.0, OP.add, -25165824.0, OP.add)
        mms((MID, R("ID"), R("M2")), (MID, R("IN2"), R("X")))
        act(R("AM"), MID, AF.Abs, 0.0, 0.5)
        lay("pL", 32, "AM", "Z16")
        lab[0] = ""
        lab[0] = "cl"
        px = R("pX", 256, 512)
        mms((px, R("ID"), R("X")), (px, R("IN"), R("AB")))
        ts(R("CLP"), px, -4.0, OP.max, 4.0, OP.min)
        lab[0] = "cn"
        pg = R("pN", 256, 512)
        mms((pg, R("IN128"), R("SGN", 0, 256)), (pg, R("IN128"), R("SGN", 256, 512)), (pg, R("IN16"), R("cH")), (pg, row("CM128", 0, 128), one(256, 1)))
        lab[0] = "ga"
        ts(R("dtf"), R("dU"), -2047.0, OP.add, 0.0625, OP.mult)
        tt(R("pE", 256, 512), R("pE", 256, 512), R("dtf"), OP.max)
        tt(R("CC", 512, 768), R("pE", 256, 512), R("c2"), OP.min)
        lab[0] = "cn"
        act(R("CN", 0, 256), pg, AF.Relu)
        lab[0] = ""
        tt(R("m3l", 0, 16), R("vF"), R("TR"), OP.subtract)
        ts(R("m3l", 32, 48), R("m3l", 0, 16), -1.0, OP.mult, float(n0 - 3584), OP.add)
        tt(R("m3l", 16, 32), R("sB", 15, 256, 16), R("NF8", 16 * s, 16 * s + 16), OP.subtract)
        tt(R("vact"), R("m3l", 0, 16), R("FL", 0, 16), OP.mult)
        tt(R("vact"), R("vact"), R("TR"), OP.add)
        tt(R("hb"), R("sB", 15, 256, 16), R("TRB"), OP.subtract)
        tt(R("a2"), R("pL", 32, 48), R("d16"), OP.min)
        scan(R("m3"), R("RS"), R("pK", 256, 512), BIG, OP.max, OP.min)
        es = R("m3", 15, 256, 16)
        tt(R("a1"), es, R("th16"), OP.min)
        tt(R("uu"), R("a2"), es, OP.min)
        tt(R("t1"), R("pL", 32, 48), R("a1"), OP.min)
        tt(R("h3", 16, 32), R("a2"), R("a1"), OP.is_le)
        tt(R("h3", 32, 48), R("th16"), R("uu"), OP.is_lt)
        tt(R("h3", 0, 16), R("d16"), R("t1"), OP.is_le)
        tt(R("FL", 16, 64), R("h3"), R("pE", 112, 160), OP.mult)
        actB, hostA, hmA, newA, nrA = [R("FL", 16 * j, 16 * j + 16) for j in range(5)]
        tt(R("p3", 16, 48), R("FL", 16, 48), R("m3l", 16, 48), OP.mult)
        tt(R("vF"), R("vF"), R("p3", 16, 32), OP.add)
        tt(R("vF"), R("vF"), R("p3", 32, 48), OP.add)
        ts(R("vS"), R("vF"), -2048.0, OP.add)
        tt(nrA, newA, R("pE", 16, 32), OP.min)
        spread("pN", 0, "BC", "vS")
        o = R("pE", 64, 112)
        o0, o1, o2 = R("pE", 64, 80), R("pE", 80, 96), R("pE", 96, 112)
        lab[0] = "sp"
        mms((o, R("ID"), R("ilB")), (o, R("ID"), R("CST")), (o0, R("I512"), actB), (o0, R("IN512"), hmA), (o0, R("IN256"), newA), (o1, R("IN512"), hmA),
            (o1, R("I512"), hostA), (o1, R("IN256"), nrA), (o2, R("IN256"), hmA), (o2, R("I512"), hostA), (o2, R("IN256"), hostA))
        lab[0] = ""
        tt(R("nrst"), R("nrst"), newA, OP.subtract)
        ts(R("w0"), hostA, 255.0, OP.mult)
        tt(R("ww"), R("nrst"), R("w0"), OP.add)
        tt(R("p3", 0, 16), hostA, R("m3l", 0, 16), OP.mult)
        tt(R("p3", 0, 16), R("vact"), R("p3", 0, 16), OP.subtract)
        tc(R("vsU"), R("p3", 0, 16))
        pairs_front()
        lab[0] = "su"
        tc(R("slU"), o)
        lab[0] = "sl"
        act(R("selc"), ind(R("CC"), R("slU", 0, 16)), AF.Copy)
        lab[0] = "cb"
        act(R("C", n0, n0 + 256), ind(R("CN"), R("slU", 32, 48)), AF.Identity, 4095.0, -16.0)
        lab[0] = "ab"
        act(R("CA", 0, 256), R("M2"), AF.Copy, 0.0, 0.5)
        act(R("A", n0, n0 + 256), ind(R("CA"), R("slU", 16, 32)), AF.Copy)
        lab[0] = ""
        pairs_count()
        tc(R("vU"), R("vF"))
        tt(R("hb"), R("hb"), hostA, OP.mult)
        ts(ind(CW, R("vsU")), R("selc"), 16.0, OP.mult, 2047.0, OP.add)
        lab[0] = "pl"
        pairs_list()
        lab[0] = ""
        if s < 7:
            children("vU" if t < 3 else "topU")
        ts(R("ap"), R("pL", 64, 80), 4096.0, OP.is_lt)
        tt(R("ap"), R("ap"), R("hb"), OP.mult)
        tt(R("ap"), R("ap"), R("TR"), OP.add)
        tc(R("asU"), R("ap"))
        tt(ind(AW, R("asU")), R("AB"), R("CLP"), OP.add)
        lab[0] = "re" if t == 3 else ""
        tt(R("OV", 16 * t, 16 * t + 16), newA, nrA, OP.subtract)
        lab[0] = ""
        if t < 3:
            ts(R("w0"), R("pL", 64, 80), 0.0, OP.is_equal)
            tt(R("FL", 0, 16), R("w0"), R("nrst"), OP.mult)
            set_act(None)

    def round_end(p):
        PK, LD = "PK%d" % p, "LD%d" % p
        lab[0] = "re"
        ts(R("rest"), R("nrst"), -1.0, OP.mult, 1.0, OP.add)
        tc(R("OV", 64, 80), R("rest"))
        scan(R("SC"), R("SCM"), R("OV"), 0.0, OP.mult, OP.add)
        mms((R("pB", 256, 336), R("BLK"), R("SC")), (R("pB", 256, 336), R("TN"), R("OV")))
        mm(R("pB", 336, 340), R("BLK"), R("SC", 15, 64, 16), True, True)
        tc(R("P5"), R("pB", 256, 336))
        ts(R("q1", 0, 64), R("P5", 0, 64), 64.0, OP.is_lt)
        tt(R("q1", 0, 64), R("q1", 0, 64), R("OV", 0, 64), OP.mult)
        tt(R("q3", 0, 64), R("P5", 0, 64), R("CT", 0, 64), OP.add)
        tt(R("q3", 0, 64), R("q3", 0, 64), R("q1", 0, 64), OP.mult)
        tt(R("q1", 0, 32), R("q3", 0, 32), R("q3", 32, 64), OP.add)
        tt(R("l1"), R("q1", 0, 16), R("q1", 16, 32), OP.add)
        tt(R("l1"), R("l1"), R("TL2"), OP.add)
        tc(R("ovU"), R("l1"))
        tc(ind(R(PK), R("ovU")), R("X"))
        ts(R(PK, 64, 320, 80), R("pB", 336, 340), 64.0, OP.min)
        tr = []
        for t in range(4):
            dst = T.cores[(rank + 1 + (4 * p + t) % (nrank - 1)) % nrank]
            e = topo.engines(core, dst)
            rid, pid, _ = topo.addr(dst)
            tr.append(RemoteDMATransfer(dst_ids=[DstId(rid=rid, pnc=pid)], dma_engine_mask=(1 << e[2 * t]) | (1 << e[2 * t + 1]), remote_sem=T.sem["ra%d" % p],
                                        srcs=[T[PK][:, 80 * t:80 * t + 80]], dsts=[T[LD][:, 80 * t:80 * t + 80]]))

        def send(q, reads, writes):
            order(q, reads, [])
            g.remote_dma_fused(tr, local_sem=T.sem.rl)
            clocks[("ra%d" % p, 8)] = {}
            acc.setdefault(LD, []).append((True, 0, 320, 1, "ra%d" % p, 8, "remote"))
        rec("g", send, [R(LD, 0, 320)], [R(PK, 0, 320)], 1500.0, 2500.0)
        lab[0] = ""
        act(R("AV"), ind(AW, R("vU")), AF.Copy)
        pn = R("pN", 0, 256)
        mms((pn, R("ID"), R("X")), (pn, R("IN"), R("AV")))
        act(R(LD, 320, 576), pn, AF.Abs)
        tc(R("cnt4", 0, 4), R(LD, 64, 320, 80))
        scan(R("cum4", 0, 4), one(4), R("cnt4", 0, 4), 0.0, OP.mult, OP.add)
        ts(R("gap4", 0, 4), R("cnt4", 0, 4), -1.0, OP.mult, 80.0, OP.add)
        nr = R("P5", 64, 80)
        for j in range(3):
            ts(R("l%d" % (j + 1)), nr, R("cum4", j, j + 1), OP.is_ge, R("gap4", j, j + 1), OP.mult)
        ts(R("l4"), nr, R("cum4", 3, 4), OP.is_lt)
        tt(R("l1"), R("l1"), R("l2"), OP.add)
        tt(R("l3"), R("l3"), nr, OP.add)
        tt(R("l1"), R("l1"), R("l3"), OP.add)
        tt(R("l4"), R("l4"), R("rest"), OP.mult)
        tt(R("l1"), R("l1"), R("TL2"), OP.subtract)
        tt(R("l1"), R("l1"), R("l4"), OP.mult)
        tt(R("l1"), R("l1"), R("TL2"), OP.add)
        tc(R("dlU"), R("l1"))
        tc(R("X"), ind(R(LD), R("dlU")))

    tc(R("vU"), R("topU"))
    tc(R("vF"), R("topF", 0, 16))
    ts(R("vS"), R("vF"), -2048.0, OP.add)
    children("topU", R("KI"))
    for p in range(2):
        if p:
            newx()
            tc(R("vU"), R("topU"))
            tc(R("vF"), R("topF", 0, 16))
            set_act(R("act0"))
        ms(R("nrst"), 1.0)
        for t in range(4):
            step(4 * p + t)
        if p:
            dma("y", T.yc[:], T.C[:, 0:3584], [], [R("C", 0, 3584)], 14000.0)
            dma("y", T.ya[:], T.A[:, 0:3584], [], [R("A", 0, 3584)], 7000.0)
        round_end(p)
    dma("y", T.yx[:], T.X[:], [], [R("X")])
    flush()
    g.wait_ge(T.sem.rl, 16)
    for i in range(6, ndma[0]):
        g.sync.wait_ge(T.sem["dm%d" % i], 16)
    for q in ("v", "t", "s", "g"):
        g.sync.wait_ge(T.sem[SEM[q]], count[SEM[q]])
